import numpy as np
import ml_dtypes


def mxq(x, axis, fmt="e4m3"):
    dtype, down = {"e4m3": (ml_dtypes.float8_e4m3fn, 7), "e5m2": (ml_dtypes.float8_e5m2, 14)}[fmt]
    v = np.moveaxis(np.asarray(x, np.float32).astype(ml_dtypes.bfloat16).astype(np.float64), axis, -1)
    blocks = v.reshape(v.shape[:-1] + (-1, 32))
    amax = np.abs(blocks).max(-1, keepdims=True)
    byte = np.maximum(np.where(amax > 0, np.frexp(amax)[1] - 1 + 127, 0) - down, 1)
    scale = np.exp2(byte - 127.0)
    codes = (blocks / scale).astype(np.float32).astype(dtype).astype(np.float64)
    return np.moveaxis((codes * scale).reshape(v.shape), -1, axis)


WIDE = False


def mx_kscale(k):
    if not WIDE:
        return np.ones(k)
    levels = np.array([10, -10, 5, -5, 0])
    if k % 512:
        return np.exp2(np.random.permutation(np.resize(levels, k // 32))).repeat(32)
    a = np.empty((k // 512, 16))
    for p in range(k // 512):
        a[p, :8] = np.random.permutation(np.resize(levels, 8))
        for g in range(8):
            far = levels[np.abs(levels - a[p, g]) >= 10]
            a[p, g + 8] = far[np.random.randint(len(far))]
    return np.exp2(a.ravel()).repeat(32)


def f64(x):
    return np.asarray(x).astype(np.float64)


def striped(idx):
    return np.tile(np.asarray(idx).reshape(-1, 16).T, (8, 1)).astype(np.uint16)


def unstriped(offs):
    return offs[:16].T.reshape(-1).astype(np.int64)


E2M1 = np.array([0.0, 0.5, 1.0, 1.5, 2.0, 3.0, 4.0, 6.0, -0.0, -0.5, -1.0, -1.5, -2.0, -3.0, -4.0, -6.0])


def pack_weight(w, fmt):
    k, n = w.shape
    w = f64(np.asarray(w, np.float32).astype(ml_dtypes.bfloat16)).reshape(k // 32, 32, n)
    amax = np.abs(w).max(1)
    if fmt == "e4m3":
        byte = np.frexp(amax)[1] - 1 + 127 - 7
    else:
        mant, ex = np.frexp(amax / 6.0)
        byte = np.where(mant > 0.5, ex, ex - 1) + 127
    byte = np.clip(np.where(amax > 0, byte, 1), 1, 254)
    scaled = (w * np.exp2(127.0 - byte)[:, None, :]).reshape(k, n).astype(np.float32)
    by_word = np.ascontiguousarray(scaled.reshape(k // 512, 128, 4, n).transpose(0, 1, 3, 2))
    if fmt == "e4m3":
        words = by_word.astype(ml_dtypes.float8_e4m3fn).view(np.uint8)
    else:
        c = by_word.astype(ml_dtypes.float4_e2m1fn).view(np.uint8) & 0xF
        words = (c[..., 0::2] | (c[..., 1::2] << 4)).reshape(k // 512, 128, 2 * n)
    return np.ascontiguousarray(words), np.ascontiguousarray(byte.astype(np.uint8).reshape(k // 512, 16, n))


def unpack_weight(words, scales, fmt):
    g, _, n = scales.shape
    words = np.ascontiguousarray(words).reshape(g, 128, n, -1)
    if fmt == "e4m3":
        vals = words.view(ml_dtypes.float8_e4m3fn).astype(np.float64)
    else:
        nib = np.empty((g, 128, n, 4), np.uint8)
        nib[..., 0::2] = words & 0xF
        nib[..., 1::2] = words >> 4
        vals = E2M1[nib]
    vals = vals * np.repeat(np.exp2(scales.astype(np.float64) - 127.0), 8, axis=1)[..., None]
    return vals.transpose(0, 1, 3, 2).reshape(g * 512, n)


def sigmoid(v):
    return 1.0 / (1.0 + np.exp(-v))


def bf(x):
    return np.asarray(x, np.float32).astype(ml_dtypes.bfloat16)


def planes(Y):
    r, m = Y.shape
    b = f64(bf(Y)).reshape(r // 32, 32, m)
    amax = np.abs(b).max(1)
    byte = np.clip(np.where(amax > 0, np.frexp(amax)[1] - 1 + 127 - 7, 1), 1, 254)
    codes = (b * np.exp2(127.0 - byte)[:, None, :]).reshape(r, m).astype(np.float32).astype(ml_dtypes.float8_e4m3fn).view(np.uint8)
    words = codes.reshape(r // 512, 128, 4, m).transpose(0, 1, 3, 2)
    return np.ascontiguousarray(words), np.ascontiguousarray(byte.astype(np.uint8).reshape(r // 512, 16, m))


D, T, I, Q, E, M = 512, 2048, 512, 256, 512, 512


def setup_inputs():
    n = np.random.standard_normal
    idx = np.random.permutation(T)[:I]
    fd = mx_kscale(D)
    fm = mx_kscale(M)
    fi = mx_kscale(I)
    ti = np.ones(T)
    ti[idx] = fi
    keysp = pack_weight(n((D, T)) / fd[:, None], "e2m1")
    return {
        "query": (n((D, Q)) * 0.4 / np.sqrt(D) * fd[:, None]).astype(np.float32),
        "pkey": (n((D, M)) / fd[:, None]).astype(np.float32),
        "pval": (n((M, E)) / fm[:, None]).astype(np.float32),
        "keys_words": keysp[0],
        "keys_scales": keysp[1],
        "vals": (n((E, T)) / ti).astype(np.float32),
        "l1": (np.random.uniform(7.0, 7.6, (Q, 1))).astype(np.float32),
        "l2": (np.random.uniform(7.0, 7.6, (Q, 1))).astype(np.float32),
        "psz": (np.random.uniform(0.5, 2.0, (1, M)) * fm).astype(np.float32),
        "size": (np.random.uniform(0.5, 2.0, (1, I)) * fi).astype(np.float32),
        "offs": striped(idx),
    }


def reference(query, pkey, pval, keys_words, keys_scales, vals, l1, l2, psz, size, offs):
    idx = unstriped(offs)
    keysu = unpack_weight(keys_words, keys_scales, "e2m1")
    queryq = mxq(f64(query), 0, "e4m3")
    pkeyq = mxq(f64(pkey), 0, "e4m3")
    a = queryq.T @ pkeyq
    keysidxg = keysu[:, idx]
    b = queryq.T @ keysidxg
    g = sigmoid(f64(l1) - f64(l2))
    w = np.exp(a - f64(l1)) * g * f64(psz)
    x = np.exp(b - f64(l2)) * (1.0 - g) * f64(size)
    wt = w.T
    xt = x.T
    vt = f64(vals)[:, idx].T
    pvalq = mxq(f64(pval), 0, "e4m3")
    wtq = mxq(wt, 0, "e4m3")
    vtq = mxq(vt, 0, "e4m3")
    xtq = mxq(xt, 0, "e4m3")
    o = pvalq.T @ wtq + vtq.T @ xtq
    words, scales = planes(o)
    return o, words, scales

@@ -1,0 +1,231 @@
+from contextlib import ExitStack
+
+import concourse.mybir as mybir
+from concourse.masks import make_identity
+
+D, T, I, Q, E, M = 512, 2048, 512, 256, 512, 512
+FLOPS = 2 * (D * Q * M + D * Q * I + M * E * Q + I * E * Q)
+
+F32 = mybir.dt.float32
+BF16 = mybir.dt.bfloat16
+I32 = mybir.dt.int32
+U32 = mybir.dt.uint32
+U16 = mybir.dt.uint16
+U8 = mybir.dt.uint8
+FP8X4 = mybir.dt.float8_e4m3fn_x4
+FP4X4 = mybir.dt.float4_e2m1fn_x4
+ALU = mybir.AluOpType
+ACT = mybir.ActivationFunctionType
+
+P = 128
+PREFIX, SUFFIX = 0, 1
+PK_SPLIT = 256
+Y_SPLIT = 160
+
+
+def tile_attend_cascade_pl_kernel(tc, query, pkey, pval, keys_words, keys_scales, vals, l1, l2, psz, size, offs,
+                                   out_0, out_1, out_2):
+    nc = tc.nc
+    with ExitStack() as ctx:
+        sb = ctx.enter_context(tc.tile_pool(name="sb", bufs=1))
+        ps_score = ctx.enter_context(tc.psum_pool(name="ps_score", bufs=2))
+        ps_spread = ctx.enter_context(tc.psum_pool(name="ps_spread", bufs=2))
+        ps_turn = ctx.enter_context(tc.psum_pool(name="ps_turn", bufs=4))
+
+        def alloc(shape, dtype, name):
+            return sb.tile(shape, dtype, name=name, align_bytes=64)
+
+        def quantize(codes, scales, values):
+            nc.vector.quantize_mx(out=codes.bitcast(FP8X4), scales=scales, in_=values)
+
+        offsets = sb.tile([P, I // 16], U16, name="offsets")
+        nc.sync.dma_start(offsets[:], offs)
+        q_raw = alloc([P, 4, Q], F32, "q_raw")
+        nc.sync.dma_start(q_raw[:], query.rearrange("(p j) q -> p j q", j=4))
+        key_words = alloc([P, T], U16, "key_words")
+        nc.sync.dma_start(key_words[:].bitcast(I32), keys_words[0].bitcast(I32))
+        pk_raw = alloc([P, 4, M], F32, "pk_raw")
+        nc.sync.dma_start(pk_raw[:], pkey.rearrange("(p j) m -> p j m", j=4))
+
+        lse = alloc([P, 2, 8], F32, "lse")
+        nc.scalar.dma_start(lse[:, PREFIX, 0:2], l1.rearrange("(p c) o -> p (c o)", c=2))
+        nc.scalar.dma_start(lse[:, SUFFIX, 0:2], l2.rearrange("(p c) o -> p (c o)", c=2))
+        token_w = alloc([P, 2, 8], F32, "token_w")
+        nc.scalar.dma_start(token_w[:, SUFFIX, 0:4], size.rearrange("o (p t) -> p (o t)", t=4))
+        nc.scalar.dma_start(token_w[:, PREFIX, 0:4], psz.rearrange("o (p t) -> p (o t)", t=4))
+
+        vals_by_r = vals.rearrange("(p r) t -> r p t", r=4)
+        val_pool = []
+        for r in range(4):
+            val_pool.append(alloc([P, T], F32, "val_pool%d" % r))
+            nc.sync.dma_start(val_pool[r][:], vals_by_r[r])
+        pval_rows = pval.rearrange("(p j) e -> p j e", j=4)
+        pv_raw = []
+        for h in range(2):
+            pv_raw.append(alloc([P, 4, E // 2], F32, "pv_raw%d" % h))
+            nc.sync.dma_start(pv_raw[h][:], pval_rows[:, :, h * (E // 2):(h + 1) * (E // 2)])
+
+        key_scales = alloc([P, T], U8, "key_scales")
+        nc.vector.memset(key_scales[:].bitcast(I32), 0)
+        for quad in range(4):
+            nc.gpsimd.dma_start(key_scales[32 * quad:32 * quad + 4, :].bitcast(I32),
+                                keys_scales[0, 4 * quad:4 * quad + 4, :].bitcast(I32))
+        ident = alloc([P, P], F32, "ident")
+        make_identity(nc, ident[:])
+
+        neg_lse = alloc([P, 2, 2], F32, "neg_lse")
+        gap = alloc([P, 2, 2], F32, "gap")
+        share = alloc([P, 2, 2], F32, "share")
+        nc.vector.tensor_sub(gap[:, PREFIX, :], lse[:, SUFFIX, 0:2], lse[:, PREFIX, 0:2])
+        nc.vector.tensor_sub(gap[:, SUFFIX, :], lse[:, PREFIX, 0:2], lse[:, SUFFIX, 0:2])
+        nc.vector.tensor_scalar_mul(neg_lse[:], lse[:, :, 0:2], -1.0)
+        odds = alloc([P, 2, 2], F32, "odds")
+        nc.scalar.activation(odds[:], gap[:], ACT.Exp)
+
+        q_bf = alloc([P, 4 * Q], BF16, "q_bf")
+        nc.vector.tensor_copy(
+            q_bf[:].rearrange("p (c a b j) -> p a j b c", c=2, b=2, j=4),
+            q_raw[:].rearrange("p j (a b c) -> p a j b c", b=2, c=2))
+        denom = alloc([P, 2, 2], F32, "denom")
+        nc.vector.tensor_scalar_add(denom[:], odds[:], 1.0)
+        q_codes = alloc([P, Q], U32, "q_codes")
+        q_scales = alloc([P, Q], U8, "q_scales")
+        quantize(q_codes[:], q_scales[:], q_bf[:])
+        nc.vector.reciprocal(share[:], denom[:])
+
+        spread = [None, None]
+        for part in (SUFFIX, PREFIX):
+            spread[part] = ps_spread.tile([P, 512], F32, name="spread")
+            by_place = spread[part][:].rearrange("q (u p e) -> q u p e", u=2, e=2)
+            for t in range(4):
+                nc.tensor.transpose(by_place[:, t // 2, :, t % 2],
+                                    token_w[:, part, t:t + 1].to_broadcast([P, P]), ident[:])
+
+        kg_words = alloc([P, I], U16, "kg_words")
+        nc.vector.tensor_copy(kg_words[:], key_words[:].indirect(offsets[:]))
+        kg_scales = alloc([P, I], U8, "kg_scales")
+        nc.vector.tensor_copy(kg_scales[:], key_scales[:].indirect(offsets[:]))
+
+        def scores_exp(part, c, rhs, rhs_scale):
+            bank = ps_score.tile([P, 512], F32, name="score")
+            nc.tensor.matmul_mx(out=bank[:], lhsT=q_codes[:, c * P:(c + 1) * P].bitcast(FP8X4),
+                                lhsT_scale=q_scales[:, c * P:(c + 1) * P], rhs=rhs, rhs_scale=rhs_scale,
+                                start=True, stop=True)
+            ex = alloc([P, 512], F32, "ex%d%d" % (part, c))
+            nc.scalar.activation(ex[:].rearrange("q (u p e) -> q u p e", u=2, e=2),
+                                 bank[:].rearrange("q (p u e) -> q u p e", u=2, e=2),
+                                 ACT.Exp, bias=neg_lse[:, part, c:c + 1])
+            return ex
+
+        pk_bf = alloc([P, 4 * M], BF16, "pk_bf")
+        pk_dst = pk_bf[:].rearrange("p (a i j) -> p a j i", i=4, j=4)
+        pk_src = pk_raw[:].rearrange("p j (a i) -> p a j i", i=4)
+        nc.scalar.copy(pk_dst[:, PK_SPLIT // 4:, :, :], pk_src[:, PK_SPLIT // 4:, :, :])
+        nc.vector.tensor_copy(pk_dst[:, :PK_SPLIT // 4, :, :], pk_src[:, :PK_SPLIT // 4, :, :])
+        ex_suffix = [scores_exp(SUFFIX, c, kg_words[:].bitcast(FP4X4), kg_scales[:]) for c in range(2)]
+        pk_codes = alloc([P, M], U32, "pk_codes")
+        pk_scales = alloc([P, M], U8, "pk_scales")
+        quantize(pk_codes[:], pk_scales[:], pk_bf[:])
+        ex_prefix = [scores_exp(PREFIX, c, pk_codes[:].bitcast(FP8X4), pk_scales[:]) for c in range(2)]
+
+        def weigh_and_turn(part, ex):
+            bank = ps_turn.tile([P, 2, 2, P], F32, name="turn")
+            for c in range(2):
+                w_rows = alloc([P, 512], BF16, "w_rows%d%d" % (part, c))
+                nc.vector.scalar_tensor_tensor(w_rows[:], ex[c][:], share[:, part, c:c + 1], spread[part][:],
+                                               ALU.mult, ALU.mult)
+                pairs = w_rows[:].bitcast(F32)
+                for u in range(2):
+                    nc.tensor.transpose(bank[:, c, u, :], pairs[:, u * P:(u + 1) * P], ident[:])
+            w_bf = alloc([P, 4 * Q], BF16, "w_bf%d" % part)
+            nc.scalar.copy(w_bf[:].bitcast(F32).rearrange("p (s c u) -> p s c u", c=2, u=2),
+                           bank[:].rearrange("p c u s -> p s c u"))
+            return w_bf
+
+        def gather_and_turn(r):
+            picked = alloc([P, I], BF16, "picked%d" % r)
+            nc.vector.tensor_copy(picked[:], val_pool[r][:].indirect(offsets[:]))
+            pairs = picked[:].bitcast(F32)
+            bank = ps_turn.tile([P, 2, P], F32, name="turn")
+            for u in range(2):
+                nc.tensor.transpose(bank[:, u, :], pairs[:, u:I // 2:2], ident[:])
+            vt_bf = alloc([P, 4 * P], BF16, "vt_bf%d" % r)
+            nc.scalar.copy(vt_bf[:].bitcast(F32).rearrange("p (s u) -> p s u", u=2),
+                           bank[:].rearrange("p u s -> p s u"))
+            return vt_bf
+
+        def quantized(values, width, name):
+            codes = alloc([P, width], U32, name + "_codes")
+            scales = alloc([P, width], U8, name + "_scales")
+            quantize(codes[:], scales[:], values[:])
+            return codes, scales
+
+        acc = []
+
+        def open_sum(r, vt, xt):
+            pool = ps_score if r < 2 else ps_spread
+            bank = pool.tile([P, Q], F32, name="score" if r < 2 else "spread")
+            nc.tensor.matmul_mx(out=bank[:], lhsT=vt[0][:].bitcast(FP8X4), lhsT_scale=vt[1][:],
+                                rhs=xt[0][:].bitcast(FP8X4), rhs_scale=xt[1][:], start=True, stop=False)
+            acc.append(bank)
+
+        vt_bf0 = gather_and_turn(0)
+        x_bf = weigh_and_turn(SUFFIX, ex_suffix)
+        vt_bf1 = gather_and_turn(1)
+        vt0 = quantized(vt_bf0, P, "vt0")
+        w_bf = weigh_and_turn(PREFIX, ex_prefix)
+        xt = quantized(x_bf, Q, "xt")
+        vt_bf2 = gather_and_turn(2)
+        vt1 = quantized(vt_bf1, P, "vt1")
+        wt = quantized(w_bf, Q, "wt")
+        open_sum(0, vt0, xt)
+        open_sum(1, vt1, xt)
+        vt2 = quantized(vt_bf2, P, "vt2")
+        open_sum(2, vt2, xt)
+        vt_bf3 = gather_and_turn(3)
+
+        pv_codes = alloc([P, 4, P], U32, "pv_codes")
+        pv_scales = alloc([P, 4, P], U8, "pv_scales")
+
+        def deal_pval(h):
+            pv_bf = alloc([P, 4, 64, 4], BF16, "pv_bf%d" % h)
+            dst = pv_bf[:].rearrange("p r s j -> p s j r")
+            src = pv_raw[h][:].rearrange("p j (s r) -> p s j r", r=4)
+            nc.scalar.copy(dst[:, :, :, 3], src[:, :, :, 3])
+            nc.vector.tensor_copy(dst[:, :, :, 0:3], src[:, :, :, 0:3])
+            return pv_bf
+
+        def quantize_pval(h, r, pv_bf):
+            quantize(pv_codes[:, r, 64 * h:64 * (h + 1)], pv_scales[:, r, 64 * h:64 * (h + 1)],
+                     pv_bf[:, r, :, :].rearrange("p s j -> p (s j)"))
+
+        pv_bf0 = deal_pval(0)
+        for r in range(4):
+            quantize_pval(0, r, pv_bf0)
+        pv_bf1 = deal_pval(1)
+        vt3 = quantized(vt_bf3, P, "vt3")
+        open_sum(3, vt3, xt)
+
+        y = alloc([P, 4, Q], F32, "y")
+        for r in range(4):
+            quantize_pval(1, r, pv_bf1)
+            nc.tensor.matmul_mx(out=acc[r][:], lhsT=pv_codes[:, r, :].bitcast(FP8X4), lhsT_scale=pv_scales[:, r, :],
+                                rhs=wt[0][:].bitcast(FP8X4), rhs_scale=wt[1][:], start=False, stop=True)
+        for r in range(4):
+            if r % 2 == 0:
+                nc.scalar.copy(y[:, r, :], acc[r][:])
+            else:
+                nc.vector.tensor_copy(y[:, r, :], acc[r][:])
+        nc.sync.dma_start(out_0.rearrange("(p r) q -> p r q", r=4), y[:])
+
+        y_bf = alloc([P, 4 * Q], BF16, "y_bf")
+        y_dst = y_bf[:].rearrange("p (a i r) -> p a r i", i=4, r=4)
+        y_src = y[:].rearrange("p r (a i) -> p a r i", i=4)
+        nc.vector.tensor_copy(y_dst[:, :Y_SPLIT // 4, :, :], y_src[:, :Y_SPLIT // 4, :, :])
+        nc.scalar.copy(y_dst[:, Y_SPLIT // 4:, :, :], y_src[:, Y_SPLIT // 4:, :, :])
+        y_codes, y_scales = quantized(y_bf, Q, "y")
+        nc.sync.dma_start(out_1[0].rearrange("p c r -> p (c r)").bitcast(I32), y_codes[:].bitcast(I32))
+        for quad in range(4):
+            queue = nc.sync if quad % 2 == 0 else nc.scalar
+            queue.dma_start(out_2[0, 4 * quad:4 * quad + 4, :].bitcast(I32),
+                            y_scales[32 * quad:32 * quad + 4, :].bitcast(I32))

@@ -19,8 +19,12 @@ ACT = mybir.ActivationFunctionType
 
 P = 128
 PREFIX, SUFFIX = 0, 1
-PK_SPLIT = 256
+PK_SPLIT = 336
 Y_SPLIT = 160
+AT_VALS = [8192 * r for r in range(4)]
+AT_PKEY = 4 * 8192
+AT_PVAL = 5 * 8192
+AT_KEY_SCALES = 6 * 8192
 
 
 def tile_attend_cascade_pl_kernel(tc, query, pkey, pval, keys_words, keys_scales, vals, l1, l2, psz, size, offs,
@@ -28,70 +32,49 @@ def tile_attend_cascade_pl_kernel(tc, query, pkey, pval, keys_words, keys_scales
     nc = tc.nc
     with ExitStack() as ctx:
         sb = ctx.enter_context(tc.tile_pool(name="sb", bufs=1))
+        reused = ctx.enter_context(tc.tile_pool(name="reused", bufs=1))
         ps_score = ctx.enter_context(tc.psum_pool(name="ps_score", bufs=2))
         ps_spread = ctx.enter_context(tc.psum_pool(name="ps_spread", bufs=2))
         ps_turn = ctx.enter_context(tc.psum_pool(name="ps_turn", bufs=4))
 
-        def alloc(shape, dtype, name):
-            return sb.tile(shape, dtype, name=name, align_bytes=64)
+        def alloc(shape, dtype, name, at=None):
+            if at is None:
+                return sb.tile(shape, dtype, name=name, align_bytes=64)
+            return reused.tile(shape, dtype, name=name, align_bytes=64, offset=at)
 
         def quantize(codes, scales, values):
             nc.vector.quantize_mx(out=codes.bitcast(FP8X4), scales=scales, in_=values)
 
         offsets = sb.tile([P, I // 16], U16, name="offsets")
         nc.sync.dma_start(offsets[:], offs)
-        q_raw = alloc([P, 4, Q], F32, "q_raw")
-        nc.sync.dma_start(q_raw[:], query.rearrange("(p j) q -> p j q", j=4))
+        lse = [alloc([P, 2], F32, "lse_prefix"), alloc([P, 2], F32, "lse_suffix")]
+        nc.sync.dma_start(lse[PREFIX][:], l1.rearrange("(p c) o -> p (c o)", c=2))
+        nc.scalar.dma_start(lse[SUFFIX][:], l2.rearrange("(p c) o -> p (c o)", c=2))
+        token_w = [alloc([P, 4], F32, "psz_cols"), alloc([P, 4], F32, "size_cols")]
+        nc.scalar.dma_start(token_w[SUFFIX][:], size.rearrange("o (p t) -> p (o t)", t=4))
+        nc.scalar.dma_start(token_w[PREFIX][:], psz.rearrange("o (p t) -> p (o t)", t=4))
         key_words = alloc([P, T], U16, "key_words")
         nc.sync.dma_start(key_words[:].bitcast(I32), keys_words[0].bitcast(I32))
-        pk_raw = alloc([P, 4, M], F32, "pk_raw")
-        nc.sync.dma_start(pk_raw[:], pkey.rearrange("(p j) m -> p j m", j=4))
-
-        lse = alloc([P, 2, 8], F32, "lse")
-        nc.scalar.dma_start(lse[:, PREFIX, 0:2], l1.rearrange("(p c) o -> p (c o)", c=2))
-        nc.scalar.dma_start(lse[:, SUFFIX, 0:2], l2.rearrange("(p c) o -> p (c o)", c=2))
-        token_w = alloc([P, 2, 8], F32, "token_w")
-        nc.scalar.dma_start(token_w[:, SUFFIX, 0:4], size.rearrange("o (p t) -> p (o t)", t=4))
-        nc.scalar.dma_start(token_w[:, PREFIX, 0:4], psz.rearrange("o (p t) -> p (o t)", t=4))
-
-        vals_by_r = vals.rearrange("(p r) t -> r p t", r=4)
-        val_pool = []
-        for r in range(4):
-            val_pool.append(alloc([P, T], F32, "val_pool%d" % r))
-            nc.sync.dma_start(val_pool[r][:], vals_by_r[r])
-        pval_rows = pval.rearrange("(p j) e -> p j e", j=4)
-        pv_raw = []
-        for h in range(2):
-            pv_raw.append(alloc([P, 4, E // 2], F32, "pv_raw%d" % h))
-            nc.sync.dma_start(pv_raw[h][:], pval_rows[:, :, h * (E // 2):(h + 1) * (E // 2)])
-
-        key_scales = alloc([P, T], U8, "key_scales")
+        q_raw = alloc([P, 4, Q], F32, "q_raw")
+        nc.sync.dma_start(q_raw[:], query.rearrange("(p j) q -> p j q", j=4))
+        key_scales = alloc([P, T], U8, "key_scales", AT_KEY_SCALES)
         nc.vector.memset(key_scales[:].bitcast(I32), 0)
         for quad in range(4):
-            nc.gpsimd.dma_start(key_scales[32 * quad:32 * quad + 4, :].bitcast(I32),
-                                keys_scales[0, 4 * quad:4 * quad + 4, :].bitcast(I32))
+            nc.sync.dma_start(key_scales[quad:P:32, :].bitcast(I32), keys_scales[0, quad:16:4, :].bitcast(I32))
+        vals_by_r = vals.rearrange("(p r) t -> r p t", r=4)
+
+        def load_vals(r):
+            pool_r = alloc([P, T], F32, "val_pool%d" % r, AT_VALS[r])
+            nc.sync.dma_start(pool_r[:], vals_by_r[r])
+            return pool_r
+
+        pk_raw = alloc([P, 4, M], F32, "pk_raw", AT_PKEY)
+        nc.sync.dma_start(pk_raw[:], pkey.rearrange("(p j) m -> p j m", j=4))
+        val_pool = [load_vals(r) for r in range(4)]
+        pv_raw = alloc([P, 4, E], F32, "pv_raw", AT_PVAL)
+        nc.sync.dma_start(pv_raw[:], pval.rearrange("(p j) e -> p j e", j=4))
         ident = alloc([P, P], F32, "ident")
         make_identity(nc, ident[:])
-
-        neg_lse = alloc([P, 2, 2], F32, "neg_lse")
-        gap = alloc([P, 2, 2], F32, "gap")
-        share = alloc([P, 2, 2], F32, "share")
-        nc.vector.tensor_sub(gap[:, PREFIX, :], lse[:, SUFFIX, 0:2], lse[:, PREFIX, 0:2])
-        nc.vector.tensor_sub(gap[:, SUFFIX, :], lse[:, PREFIX, 0:2], lse[:, SUFFIX, 0:2])
-        nc.vector.tensor_scalar_mul(neg_lse[:], lse[:, :, 0:2], -1.0)
-        odds = alloc([P, 2, 2], F32, "odds")
-        nc.scalar.activation(odds[:], gap[:], ACT.Exp)
-
-        q_bf = alloc([P, 4 * Q], BF16, "q_bf")
-        nc.vector.tensor_copy(
-            q_bf[:].rearrange("p (c a b j) -> p a j b c", c=2, b=2, j=4),
-            q_raw[:].rearrange("p j (a b c) -> p a j b c", b=2, c=2))
-        denom = alloc([P, 2, 2], F32, "denom")
-        nc.vector.tensor_scalar_add(denom[:], odds[:], 1.0)
-        q_codes = alloc([P, Q], U32, "q_codes")
-        q_scales = alloc([P, Q], U8, "q_scales")
-        quantize(q_codes[:], q_scales[:], q_bf[:])
-        nc.vector.reciprocal(share[:], denom[:])
 
         spread = [None, None]
         for part in (SUFFIX, PREFIX):
@@ -99,39 +82,48 @@ def tile_attend_cascade_pl_kernel(tc, query, pkey, pval, keys_words, keys_scales
             by_place = spread[part][:].rearrange("q (u p e) -> q u p e", u=2, e=2)
             for t in range(4):
                 nc.tensor.transpose(by_place[:, t // 2, :, t % 2],
-                                    token_w[:, part, t:t + 1].to_broadcast([P, P]), ident[:])
+                                    token_w[part][:, t:t + 1].to_broadcast([P, P]), ident[:])
+
+        neg_lse = alloc([P, 2, 2], F32, "neg_lse")
+        gap = alloc([P, 2, 2], F32, "gap")
+        share = alloc([P, 2, 2], F32, "share")
+        for part in (PREFIX, SUFFIX):
+            nc.vector.tensor_sub(gap[:, part, :], lse[1 - part][:], lse[part][:])
+            nc.vector.tensor_scalar_mul(neg_lse[:, part, :], lse[part][:], -1.0)
+        odds = alloc([P, 2, 2], F32, "odds")
+        nc.scalar.activation(odds[:], gap[:], ACT.Exp)
 
         kg_words = alloc([P, I], U16, "kg_words")
         nc.vector.tensor_copy(kg_words[:], key_words[:].indirect(offsets[:]))
+        denom = alloc([P, 2, 2], F32, "denom")
+        nc.vector.tensor_scalar_add(denom[:], odds[:], 1.0)
         kg_scales = alloc([P, I], U8, "kg_scales")
         nc.vector.tensor_copy(kg_scales[:], key_scales[:].indirect(offsets[:]))
 
-        def scores_exp(part, c, rhs, rhs_scale):
+        q_bf = alloc([P, 4 * Q], BF16, "q_bf")
+        nc.scalar.copy(
+            q_bf[:].rearrange("p (c a b j) -> p a j b c", c=2, b=2, j=4),
+            q_raw[:].rearrange("p j (a b c) -> p a j b c", b=2, c=2))
+        q_codes = alloc([P, Q], U32, "q_codes", AT_KEY_SCALES)
+        q_scales = alloc([P, Q], U8, "q_scales")
+        quantize(q_codes[:], q_scales[:], q_bf[:])
+        nc.vector.reciprocal(share[:], denom[:])
+
+        def scores_exp(part, c, rhs, rhs_scale, at=None):
             bank = ps_score.tile([P, 512], F32, name="score")
             nc.tensor.matmul_mx(out=bank[:], lhsT=q_codes[:, c * P:(c + 1) * P].bitcast(FP8X4),
                                 lhsT_scale=q_scales[:, c * P:(c + 1) * P], rhs=rhs, rhs_scale=rhs_scale,
                                 start=True, stop=True)
-            ex = alloc([P, 512], F32, "ex%d%d" % (part, c))
+            ex = alloc([P, 512], F32, "ex%d%d" % (part, c), at)
             nc.scalar.activation(ex[:].rearrange("q (u p e) -> q u p e", u=2, e=2),
                                  bank[:].rearrange("q (p u e) -> q u p e", u=2, e=2),
                                  ACT.Exp, bias=neg_lse[:, part, c:c + 1])
             return ex
 
-        pk_bf = alloc([P, 4 * M], BF16, "pk_bf")
-        pk_dst = pk_bf[:].rearrange("p (a i j) -> p a j i", i=4, j=4)
-        pk_src = pk_raw[:].rearrange("p j (a i) -> p a j i", i=4)
-        nc.scalar.copy(pk_dst[:, PK_SPLIT // 4:, :, :], pk_src[:, PK_SPLIT // 4:, :, :])
-        nc.vector.tensor_copy(pk_dst[:, :PK_SPLIT // 4, :, :], pk_src[:, :PK_SPLIT // 4, :, :])
-        ex_suffix = [scores_exp(SUFFIX, c, kg_words[:].bitcast(FP4X4), kg_scales[:]) for c in range(2)]
-        pk_codes = alloc([P, M], U32, "pk_codes")
-        pk_scales = alloc([P, M], U8, "pk_scales")
-        quantize(pk_codes[:], pk_scales[:], pk_bf[:])
-        ex_prefix = [scores_exp(PREFIX, c, pk_codes[:].bitcast(FP8X4), pk_scales[:]) for c in range(2)]
-
-        def weigh_and_turn(part, ex):
+        def weigh_and_turn(part, ex, slots):
             bank = ps_turn.tile([P, 2, 2, P], F32, name="turn")
             for c in range(2):
-                w_rows = alloc([P, 512], BF16, "w_rows%d%d" % (part, c))
+                w_rows = alloc([P, 512], BF16, "w_rows%d%d" % (part, c), slots[c])
                 nc.vector.scalar_tensor_tensor(w_rows[:], ex[c][:], share[:, part, c:c + 1], spread[part][:],
                                                ALU.mult, ALU.mult)
                 pairs = w_rows[:].bitcast(F32)
@@ -149,13 +141,15 @@ def tile_attend_cascade_pl_kernel(tc, query, pkey, pval, keys_words, keys_scales
             bank = ps_turn.tile([P, 2, P], F32, name="turn")
             for u in range(2):
                 nc.tensor.transpose(bank[:, u, :], pairs[:, u:I // 2:2], ident[:])
-            vt_bf = alloc([P, 4 * P], BF16, "vt_bf%d" % r)
-            nc.scalar.copy(vt_bf[:].bitcast(F32).rearrange("p (s u) -> p s u", u=2),
-                           bank[:].rearrange("p u s -> p s u"))
+            return bank
+
+        def weave(copy, r, bank, at=None):
+            vt_bf = alloc([P, 4 * P], BF16, "vt_bf%d" % r, at)
+            copy(vt_bf[:].bitcast(F32).rearrange("p (s u) -> p s u", u=2), bank[:].rearrange("p u s -> p s u"))
             return vt_bf
 
-        def quantized(values, width, name):
-            codes = alloc([P, width], U32, name + "_codes")
+        def quantized(values, width, name, slot=None):
+            codes = alloc([P, width], U32, name + "_codes", slot)
             scales = alloc([P, width], U8, name + "_scales")
             quantize(codes[:], scales[:], values[:])
             return codes, scales
@@ -169,53 +163,53 @@ def tile_attend_cascade_pl_kernel(tc, query, pkey, pval, keys_words, keys_scales
                                 rhs=xt[0][:].bitcast(FP8X4), rhs_scale=xt[1][:], start=True, stop=False)
             acc.append(bank)
 
-        vt_bf0 = gather_and_turn(0)
-        x_bf = weigh_and_turn(SUFFIX, ex_suffix)
-        vt_bf1 = gather_and_turn(1)
+        def close_sum(r, vt, xt):
+            nc.tensor.matmul_mx(out=acc[r][:], lhsT=vt[0][:].bitcast(FP8X4), lhsT_scale=vt[1][:],
+                                rhs=xt[0][:].bitcast(FP8X4), rhs_scale=xt[1][:], start=False, stop=True)
+
+        pk_bf = alloc([P, 4 * M], BF16, "pk_bf")
+        pk_dst = pk_bf[:].rearrange("p (a i j) -> p a j i", i=4, j=4)
+        pk_src = pk_raw[:].rearrange("p j (a i) -> p a j i", i=4)
+        nc.vector.tensor_copy(pk_dst[:, :PK_SPLIT // 4, :, :], pk_src[:, :PK_SPLIT // 4, :, :])
+        nc.scalar.copy(pk_dst[:, PK_SPLIT // 4:, :, :], pk_src[:, PK_SPLIT // 4:, :, :])
+        ex_suffix = [scores_exp(SUFFIX, c, kg_words[:].bitcast(FP4X4), kg_scales[:], AT_PKEY + 2048 * c)
+                     for c in range(2)]
+        pk = quantized(pk_bf, M, "pk")
+        ex_prefix = [scores_exp(PREFIX, c, pk[0][:].bitcast(FP8X4), pk[1][:]) for c in range(2)]
+        vt_bf0 = weave(nc.scalar.copy, 0, gather_and_turn(0))
+        x_bf = weigh_and_turn(SUFFIX, ex_suffix, (AT_VALS[0], None))
         vt0 = quantized(vt_bf0, P, "vt0")
-        w_bf = weigh_and_turn(PREFIX, ex_prefix)
-        xt = quantized(x_bf, Q, "xt")
-        vt_bf2 = gather_and_turn(2)
-        vt1 = quantized(vt_bf1, P, "vt1")
-        wt = quantized(w_bf, Q, "wt")
+        vt_bf1 = weave(nc.scalar.copy, 1, gather_and_turn(1))
+        w_bf = weigh_and_turn(PREFIX, ex_prefix, (AT_VALS[1], None))
+        xt = quantized(x_bf, Q, "xt", AT_VALS[1] + 4096)
         open_sum(0, vt0, xt)
-        open_sum(1, vt1, xt)
-        vt2 = quantized(vt_bf2, P, "vt2")
-        open_sum(2, vt2, xt)
-        vt_bf3 = gather_and_turn(3)
-
-        pv_codes = alloc([P, 4, P], U32, "pv_codes")
-        pv_scales = alloc([P, 4, P], U8, "pv_scales")
-
-        def deal_pval(h):
-            pv_bf = alloc([P, 4, 64, 4], BF16, "pv_bf%d" % h)
-            dst = pv_bf[:].rearrange("p r s j -> p s j r")
-            src = pv_raw[h][:].rearrange("p j (s r) -> p s j r", r=4)
-            nc.scalar.copy(dst[:, :, :, 3], src[:, :, :, 3])
-            nc.vector.tensor_copy(dst[:, :, :, 0:3], src[:, :, :, 0:3])
-            return pv_bf
-
-        def quantize_pval(h, r, pv_bf):
-            quantize(pv_codes[:, r, 64 * h:64 * (h + 1)], pv_scales[:, r, 64 * h:64 * (h + 1)],
-                     pv_bf[:, r, :, :].rearrange("p s j -> p (s j)"))
-
-        pv_bf0 = deal_pval(0)
-        for r in range(4):
-            quantize_pval(0, r, pv_bf0)
-        pv_bf1 = deal_pval(1)
-        vt3 = quantized(vt_bf3, P, "vt3")
-        open_sum(3, vt3, xt)
+        open_sum(1, quantized(vt_bf1, P, "vt1"), xt)
+        vt_bf2 = weave(nc.scalar.copy, 2, gather_and_turn(2))
+        wt = quantized(w_bf, Q, "wt", AT_VALS[2])
+        turned3 = gather_and_turn(3)
+        open_sum(2, quantized(vt_bf2, P, "vt2", AT_VALS[3]), xt)
+        pv_bf = alloc([P, 4, P, 4], BF16, "pv_bf")
+        pv_dst = pv_bf[:].rearrange("p r s j -> p s j r")
+        pv_src = pv_raw[:].rearrange("p j (s r) -> p s j r", r=4)
+        nc.vector.tensor_copy(pv_dst[:, :, :, 0:2], pv_src[:, :, :, 0:2])
+        nc.scalar.copy(pv_dst[:, :, :, 2:4], pv_src[:, :, :, 2:4])
+        vt_bf3 = weave(nc.scalar.copy, 3, turned3, AT_PVAL)
 
         y = alloc([P, 4, Q], F32, "y")
         for r in range(4):
-            quantize_pval(1, r, pv_bf1)
-            nc.tensor.matmul_mx(out=acc[r][:], lhsT=pv_codes[:, r, :].bitcast(FP8X4), lhsT_scale=pv_scales[:, r, :],
-                                rhs=wt[0][:].bitcast(FP8X4), rhs_scale=wt[1][:], start=False, stop=True)
-        for r in range(4):
-            if r % 2 == 0:
-                nc.scalar.copy(y[:, r, :], acc[r][:])
+            pv_codes = alloc([P, P], U32, "pv_codes%d" % r)
+            pv_scales = alloc([P, P], U8, "pv_scales%d" % r)
+            quantize(pv_codes[:], pv_scales[:], pv_bf[:, r, :, :].rearrange("p s j -> p (s j)"))
+            if r < 3:
+                close_sum(r, (pv_codes, pv_scales), wt)
             else:
+                open_sum(r, (pv_codes, pv_scales), wt)
+        close_sum(3, quantized(vt_bf3, P, "vt3"), xt)
+        for r in range(4):
+            if r == 2:
                 nc.vector.tensor_copy(y[:, r, :], acc[r][:])
+            else:
+                nc.scalar.copy(y[:, r, :], acc[r][:])
         nc.sync.dma_start(out_0.rearrange("(p r) q -> p r q", r=4), y[:])
 
         y_bf = alloc([P, 4 * Q], BF16, "y_bf")
@@ -226,6 +220,5 @@ def tile_attend_cascade_pl_kernel(tc, query, pkey, pval, keys_words, keys_scales
         y_codes, y_scales = quantized(y_bf, Q, "y")
         nc.sync.dma_start(out_1[0].rearrange("p c r -> p (c r)").bitcast(I32), y_codes[:].bitcast(I32))
         for quad in range(4):
-            queue = nc.sync if quad % 2 == 0 else nc.scalar
-            queue.dma_start(out_2[0, 4 * quad:4 * quad + 4, :].bitcast(I32),
-                            y_scales[32 * quad:32 * quad + 4, :].bitcast(I32))
+            queue = nc.scalar if quad % 2 == 0 else nc.sync
+            queue.dma_start(out_2[0, quad:16:4, :].bitcast(I32), y_scales[quad:P:32, :].bitcast(I32))

@@ -20,11 +20,17 @@ ACT = mybir.ActivationFunctionType
 P = 128
 PREFIX, SUFFIX = 0, 1
 PK_SPLIT = 336
+BANK_SCORE = [0, 1]
+BANK_WEIGHTS = [[4, 5], [2, 3]]
+BANK_VALS = [6, 7, 2, 3]
+BANK_SUM = [0, 1, 6, 4]
+GUESS = 0.9375
 Y_SPLIT = 160
 AT_VALS = [8192 * r for r in range(4)]
 AT_PKEY = 4 * 8192
 AT_PVAL = 5 * 8192
 AT_KEY_SCALES = 6 * 8192
+AT_EX = 6 * 8192 + 2048
 
 
 def tile_attend_cascade_pl_kernel(tc, query, pkey, pval, keys_words, keys_scales, vals, l1, l2, psz, size, offs,
@@ -33,9 +39,10 @@ def tile_attend_cascade_pl_kernel(tc, query, pkey, pval, keys_words, keys_scales
     with ExitStack() as ctx:
         sb = ctx.enter_context(tc.tile_pool(name="sb", bufs=1))
         reused = ctx.enter_context(tc.tile_pool(name="reused", bufs=1))
-        ps_score = ctx.enter_context(tc.psum_pool(name="ps_score", bufs=2))
-        ps_spread = ctx.enter_context(tc.psum_pool(name="ps_spread", bufs=2))
-        ps_turn = ctx.enter_context(tc.psum_pool(name="ps_turn", bufs=4))
+        psum = ctx.enter_context(tc.psum_pool(name="psum", bufs=1))
+
+        def in_bank(bank, shape, name):
+            return psum.tile(shape, F32, name=name, offset=2048 * bank)
 
         def alloc(shape, dtype, name, at=None):
             if at is None:
@@ -48,11 +55,9 @@ def tile_attend_cascade_pl_kernel(tc, query, pkey, pval, keys_words, keys_scales
         offsets = sb.tile([P, I // 16], U16, name="offsets")
         nc.sync.dma_start(offsets[:], offs)
         lse = [alloc([P, 2], F32, "lse_prefix"), alloc([P, 2], F32, "lse_suffix")]
-        nc.sync.dma_start(lse[PREFIX][:], l1.rearrange("(p c) o -> p (c o)", c=2))
+        nc.scalar.dma_start(lse[PREFIX][:], l1.rearrange("(p c) o -> p (c o)", c=2))
         nc.scalar.dma_start(lse[SUFFIX][:], l2.rearrange("(p c) o -> p (c o)", c=2))
         token_w = [alloc([P, 4], F32, "psz_cols"), alloc([P, 4], F32, "size_cols")]
-        nc.scalar.dma_start(token_w[SUFFIX][:], size.rearrange("o (p t) -> p (o t)", t=4))
-        nc.scalar.dma_start(token_w[PREFIX][:], psz.rearrange("o (p t) -> p (o t)", t=4))
         key_words = alloc([P, T], U16, "key_words")
         nc.sync.dma_start(key_words[:].bitcast(I32), keys_words[0].bitcast(I32))
         q_raw = alloc([P, 4, Q], F32, "q_raw")
@@ -70,33 +75,47 @@ def tile_attend_cascade_pl_kernel(tc, query, pkey, pval, keys_words, keys_scales
 
         pk_raw = alloc([P, 4, M], F32, "pk_raw", AT_PKEY)
         nc.sync.dma_start(pk_raw[:], pkey.rearrange("(p j) m -> p j m", j=4))
-        val_pool = [load_vals(r) for r in range(4)]
-        pv_raw = alloc([P, 4, E], F32, "pv_raw", AT_PVAL)
-        nc.sync.dma_start(pv_raw[:], pval.rearrange("(p j) e -> p j e", j=4))
+        val_pool = [load_vals(0)]
+        nc.sync.dma_start(token_w[SUFFIX][:], size.rearrange("o (p t) -> p (o t)", t=4))
+        val_pool.append(load_vals(1))
+        nc.sync.dma_start(token_w[PREFIX][:], psz.rearrange("o (p t) -> p (o t)", t=4))
+        val_pool.extend([load_vals(r) for r in range(2, 4)])
+        pv_raw = []
+        for h in range(2):
+            half = alloc([P, 4, E // 2], F32, "pv_raw%d" % h, AT_PVAL + 4096 * h)
+            nc.sync.dma_start(half[:], pval.rearrange("(p j) e -> p j e", j=4)[:, :, h * E // 2:(h + 1) * E // 2])
+            pv_raw.append(half)
         ident = alloc([P, P], F32, "ident")
         make_identity(nc, ident[:])
 
-        spread = [None, None]
-        for part in (SUFFIX, PREFIX):
-            spread[part] = ps_spread.tile([P, 512], F32, name="spread")
-            by_place = spread[part][:].rearrange("q (u p e) -> q u p e", u=2, e=2)
-            for t in range(4):
-                nc.tensor.transpose(by_place[:, t // 2, :, t % 2],
-                                    token_w[part][:, t:t + 1].to_broadcast([P, P]), ident[:])
+        def small(name):
+            return alloc([P, 2], F32, name)
 
-        neg_lse = alloc([P, 2, 2], F32, "neg_lse")
-        gap = alloc([P, 2, 2], F32, "gap")
-        share = alloc([P, 2, 2], F32, "share")
-        for part in (PREFIX, SUFFIX):
-            nc.vector.tensor_sub(gap[:, part, :], lse[1 - part][:], lse[part][:])
-            nc.vector.tensor_scalar_mul(neg_lse[:, part, :], lse[part][:], -1.0)
-        odds = alloc([P, 2, 2], F32, "odds")
-        nc.scalar.activation(odds[:], gap[:], ACT.Exp)
+        top, low, below, rest = small("top"), small("low"), small("below"), small("rest")
+        nc.vector.tensor_tensor(top[:], lse[PREFIX][:], lse[SUFFIX][:], ALU.max)
+        nc.vector.tensor_tensor(low[:], lse[PREFIX][:], lse[SUFFIX][:], ALU.min)
+        nc.vector.tensor_scalar(rest[:], top[:], -1.0, 1.0, ALU.mult, ALU.add)
+        nc.vector.tensor_sub(below[:], low[:], top[:])
+        ratio, square, slope = small("ratio"), small("square"), small("slope")
+        nc.scalar.activation(ratio[:], below[:], ACT.Exp)
+        nc.scalar.activation(square[:], ratio[:], ACT.Square, scale=0.5, bias=-GUESS)
+        nc.scalar.activation(slope[:], ratio[:], ACT.Identity, scale=-1.0, bias=-1.0)
+        back0, keep0, step1 = small("back0"), small("keep0"), small("step1")
+        nc.scalar.activation(back0[:], square[:], ACT.Exp, bias=-GUESS * GUESS)
+        nc.scalar.activation(keep0[:], square[:], ACT.Identity, bias=1.0 - GUESS * GUESS)
+        for c in range(2):
+            nc.scalar.activation(step1[:, c:c + 1], back0[:, c:c + 1], ACT.Identity,
+                                 scale=slope[:, c:c + 1], bias=keep0[:, c:c + 1])
+        back1, keep1, neg_lse = small("back1"), small("keep1"), small("neg_lse")
+        nc.scalar.activation(back1[:], step1[:], ACT.Exp)
+        for c in range(2):
+            nc.scalar.activation(keep1[:, c:c + 1], step1[:, c:c + 1], ACT.Identity, bias=rest[:, c:c + 1])
+        for c in range(2):
+            nc.scalar.activation(neg_lse[:, c:c + 1], back1[:, c:c + 1], ACT.Identity,
+                                 scale=slope[:, c:c + 1], bias=keep1[:, c:c + 1])
 
         kg_words = alloc([P, I], U16, "kg_words")
         nc.vector.tensor_copy(kg_words[:], key_words[:].indirect(offsets[:]))
-        denom = alloc([P, 2, 2], F32, "denom")
-        nc.vector.tensor_scalar_add(denom[:], odds[:], 1.0)
         kg_scales = alloc([P, I], U8, "kg_scales")
         nc.vector.tensor_copy(kg_scales[:], key_scales[:].indirect(offsets[:]))
 
@@ -107,44 +126,70 @@ def tile_attend_cascade_pl_kernel(tc, query, pkey, pval, keys_words, keys_scales
         q_codes = alloc([P, Q], U32, "q_codes", AT_KEY_SCALES)
         q_scales = alloc([P, Q], U8, "q_scales")
         quantize(q_codes[:], q_scales[:], q_bf[:])
-        nc.vector.reciprocal(share[:], denom[:])
 
         def scores_exp(part, c, rhs, rhs_scale, at=None):
-            bank = ps_score.tile([P, 512], F32, name="score")
+            bank = in_bank(BANK_SCORE[c], [P, 512], "score%d%d" % (part, c))
             nc.tensor.matmul_mx(out=bank[:], lhsT=q_codes[:, c * P:(c + 1) * P].bitcast(FP8X4),
                                 lhsT_scale=q_scales[:, c * P:(c + 1) * P], rhs=rhs, rhs_scale=rhs_scale,
                                 start=True, stop=True)
             ex = alloc([P, 512], F32, "ex%d%d" % (part, c), at)
-            nc.scalar.activation(ex[:].rearrange("q (u p e) -> q u p e", u=2, e=2),
-                                 bank[:].rearrange("q (p u e) -> q u p e", u=2, e=2),
-                                 ACT.Exp, bias=neg_lse[:, part, c:c + 1])
+            nc.scalar.activation(ex[:].rearrange("q (t p) -> q t p", t=4),
+                                 bank[:].rearrange("q (p t) -> q t p", t=4),
+                                 ACT.Exp, bias=neg_lse[:, c:c + 1])
             return ex
 
-        def weigh_and_turn(part, ex, slots):
-            bank = ps_turn.tile([P, 2, 2, P], F32, name="turn")
-            for c in range(2):
-                w_rows = alloc([P, 512], BF16, "w_rows%d%d" % (part, c), slots[c])
-                nc.vector.scalar_tensor_tensor(w_rows[:], ex[c][:], share[:, part, c:c + 1], spread[part][:],
-                                               ALU.mult, ALU.mult)
-                pairs = w_rows[:].bitcast(F32)
-                for u in range(2):
-                    nc.tensor.transpose(bank[:, c, u, :], pairs[:, u * P:(u + 1) * P], ident[:])
-            w_bf = alloc([P, 4 * Q], BF16, "w_bf%d" % part)
-            nc.scalar.copy(w_bf[:].bitcast(F32).rearrange("p (s c u) -> p s c u", c=2, u=2),
-                           bank[:].rearrange("p c u s -> p s c u"))
+        def turn_and_weigh(part, ex, at=None):
+            pairs = alloc([P, 2, Q, 2], BF16, "pairs%d" % part, at)
+            for u in range(2):
+                bank = in_bank(BANK_WEIGHTS[part][u], [P, 2, Q], "turned%d%d" % (part, u))
+                for c in range(2):
+                    for e in range(2):
+                        t = 2 * u + e
+                        nc.tensor.transpose(bank[:, e, c * P:(c + 1) * P], ex[c][:, t * P:(t + 1) * P], ident[:])
+                for e in range(2):
+                    t = 2 * u + e
+                    nc.scalar.activation(pairs[:, u, :, e], bank[:, e, :], ACT.Copy, scale=token_w[part][:, t:t + 1])
+            return pairs
+
+        def merge(part, pairs, at=None):
+            w_bf = alloc([P, 4 * Q], BF16, "w_bf%d" % part, at)
+            nc.vector.tensor_copy(w_bf[:].bitcast(F32).rearrange("p (q u) -> p q u", u=2),
+                                  pairs[:].rearrange("p u q e -> p (u q e)").bitcast(F32).rearrange(
+                                      "p (u q) -> p q u", u=2))
             return w_bf
+
+        def turn_rows(part, c, ex):
+            bank = in_bank(BANK_WEIGHTS[part][c], [P, 4, P], "turned%d%d" % (part, c))
+            for t in range(4):
+                nc.tensor.transpose(bank[:, t, :], ex[:, t * P:(t + 1) * P], ident[:])
+            return bank
+
+        def weigh_on_vector(part, banks):
+            halves = []
+            for c, bank in enumerate(banks):
+                half = alloc([P, P, 4], BF16, "w_half%d%d" % (part, c))
+                nc.vector.tensor_tensor(half[:], bank[:].rearrange("p t s -> p s t"),
+                                        token_w[part][:].unsqueeze(1).to_broadcast([P, P, 4]), ALU.mult)
+                halves.append(half)
+            codes = alloc([P, Q], U32, "w_codes%d" % part)
+            scales = alloc([P, Q], U8, "w_scales%d" % part)
+            for c in range(2):
+                quantize(codes[:, c * P:(c + 1) * P], scales[:, c * P:(c + 1) * P],
+                         halves[c][:].rearrange("p s t -> p (s t)"))
+            return codes, scales
 
         def gather_and_turn(r):
             picked = alloc([P, I], BF16, "picked%d" % r)
             nc.vector.tensor_copy(picked[:], val_pool[r][:].indirect(offsets[:]))
             pairs = picked[:].bitcast(F32)
-            bank = ps_turn.tile([P, 2, P], F32, name="turn")
+            bank = in_bank(BANK_VALS[r], [P, 2, P], "turned_vals%d" % r)
             for u in range(2):
                 nc.tensor.transpose(bank[:, u, :], pairs[:, u:I // 2:2], ident[:])
             return bank
 
-        def weave(copy, r, bank, at=None):
-            vt_bf = alloc([P, 4 * P], BF16, "vt_bf%d" % r, at)
+        def weave(copy, r, bank, at=None, vt_bf=None):
+            if vt_bf is None:
+                vt_bf = alloc([P, 4 * P], BF16, "vt_bf%d" % r, at)
             copy(vt_bf[:].bitcast(F32).rearrange("p (s u) -> p s u", u=2), bank[:].rearrange("p u s -> p s u"))
             return vt_bf
 
@@ -157,8 +202,7 @@ def tile_attend_cascade_pl_kernel(tc, query, pkey, pval, keys_words, keys_scales
         acc = []
 
         def open_sum(r, vt, xt):
-            pool = ps_score if r < 2 else ps_spread
-            bank = pool.tile([P, Q], F32, name="score" if r < 2 else "spread")
+            bank = in_bank(BANK_SUM[r], [P, Q], "sum%d" % r)
             nc.tensor.matmul_mx(out=bank[:], lhsT=vt[0][:].bitcast(FP8X4), lhsT_scale=vt[1][:],
                                 rhs=xt[0][:].bitcast(FP8X4), rhs_scale=xt[1][:], start=True, stop=False)
             acc.append(bank)
@@ -174,43 +218,48 @@ def tile_attend_cascade_pl_kernel(tc, query, pkey, pval, keys_words, keys_scales
         nc.scalar.copy(pk_dst[:, PK_SPLIT // 4:, :, :], pk_src[:, PK_SPLIT // 4:, :, :])
         ex_suffix = [scores_exp(SUFFIX, c, kg_words[:].bitcast(FP4X4), kg_scales[:], AT_PKEY + 2048 * c)
                      for c in range(2)]
+        turned_suffix = [turn_rows(SUFFIX, c, ex_suffix[c]) for c in range(2)]
         pk = quantized(pk_bf, M, "pk")
         ex_prefix = [scores_exp(PREFIX, c, pk[0][:].bitcast(FP8X4), pk[1][:]) for c in range(2)]
-        vt_bf0 = weave(nc.scalar.copy, 0, gather_and_turn(0))
-        x_bf = weigh_and_turn(SUFFIX, ex_suffix, (AT_VALS[0], None))
-        vt0 = quantized(vt_bf0, P, "vt0")
-        vt_bf1 = weave(nc.scalar.copy, 1, gather_and_turn(1))
-        w_bf = weigh_and_turn(PREFIX, ex_prefix, (AT_VALS[1], None))
-        xt = quantized(x_bf, Q, "xt", AT_VALS[1] + 4096)
-        open_sum(0, vt0, xt)
-        open_sum(1, quantized(vt_bf1, P, "vt1"), xt)
-        vt_bf2 = weave(nc.scalar.copy, 2, gather_and_turn(2))
-        wt = quantized(w_bf, Q, "wt", AT_VALS[2])
+        vt_bf01 = alloc([P, 8 * P], BF16, "vt_bf01")
+        weave(nc.scalar.copy, 0, gather_and_turn(0), None, vt_bf01[:, :4 * P])
+        xt = weigh_on_vector(SUFFIX, turned_suffix)
+        turned1 = gather_and_turn(1)
+        w_pairs = turn_and_weigh(PREFIX, ex_prefix, AT_EX)
+        weave(nc.scalar.copy, 1, turned1, None, vt_bf01[:, 4 * P:])
+        turned2 = gather_and_turn(2)
+        w_bf = merge(PREFIX, w_pairs, AT_VALS[2])
+        vt01 = quantized(vt_bf01, 2 * P, "vt01", AT_VALS[2] + 2048)
+        for r in range(2):
+            open_sum(r, (vt01[0][:, r * P:(r + 1) * P], vt01[1][:, r * P:(r + 1) * P]), xt)
+        vt_bf2 = weave(nc.scalar.copy, 2, turned2)
         turned3 = gather_and_turn(3)
+        wt = quantized(w_bf, Q, "wt", AT_VALS[3] + 1024)
         open_sum(2, quantized(vt_bf2, P, "vt2", AT_VALS[3]), xt)
+
+        pv_src = [half[:].rearrange("p j (s r) -> p s j r", r=4) for half in pv_raw]
         pv_bf = alloc([P, 4, P, 4], BF16, "pv_bf")
         pv_dst = pv_bf[:].rearrange("p r s j -> p s j r")
-        pv_src = pv_raw[:].rearrange("p j (s r) -> p s j r", r=4)
-        nc.vector.tensor_copy(pv_dst[:, :, :, 0:2], pv_src[:, :, :, 0:2])
-        nc.scalar.copy(pv_dst[:, :, :, 2:4], pv_src[:, :, :, 2:4])
-        vt_bf3 = weave(nc.scalar.copy, 3, turned3, AT_PVAL)
+        nc.scalar.copy(pv_dst[:, :P // 2], pv_src[0])
+        nc.scalar.copy(pv_dst[:, P // 2:, :, 0:2], pv_src[1][:, :, :, 0:2])
+        nc.vector.tensor_copy(pv_dst[:, P // 2:, :, 2:4], pv_src[1][:, :, :, 2:4])
+        vt_bf3 = weave(nc.scalar.copy, 3, turned3, AT_PVAL + 4096)
 
         y = alloc([P, 4, Q], F32, "y")
-        for r in range(4):
-            pv_codes = alloc([P, P], U32, "pv_codes%d" % r)
-            pv_scales = alloc([P, P], U8, "pv_scales%d" % r)
-            quantize(pv_codes[:], pv_scales[:], pv_bf[:, r, :, :].rearrange("p s j -> p (s j)"))
-            if r < 3:
-                close_sum(r, (pv_codes, pv_scales), wt)
-            else:
-                open_sum(r, (pv_codes, pv_scales), wt)
+        out_by_r = out_0.rearrange("(p r) q -> p r q", r=4)
+        def pv_operand(r):
+            return quantized(pv_bf[:, r, :, :].rearrange("p s j -> p (s j)"), P, "pv%d" % r)
+
+        close_sum(0, pv_operand(0), wt)
+        close_sum(1, pv_operand(1), wt)
+        close_sum(2, pv_operand(2), wt)
+        open_sum(3, pv_operand(3), wt)
         close_sum(3, quantized(vt_bf3, P, "vt3"), xt)
         for r in range(4):
-            if r == 2:
-                nc.vector.tensor_copy(y[:, r, :], acc[r][:])
-            else:
-                nc.scalar.copy(y[:, r, :], acc[r][:])
-        nc.sync.dma_start(out_0.rearrange("(p r) q -> p r q", r=4), y[:])
+            copy = nc.vector.tensor_copy if r == 2 else nc.scalar.copy
+            copy(y[:, r, :].rearrange("p (s c) -> p s c", c=2), acc[r][:].rearrange("p (c s) -> p s c", c=2))
+            if r % 2 == 1:
+                nc.sync.dma_start(out_by_r[:, r - 1:r + 1, :], y[:, r - 1:r + 1, :])
 
         y_bf = alloc([P, 4 * Q], BF16, "y_bf")
         y_dst = y_bf[:].rearrange("p (a i r) -> p a r i", i=4, r=4)

@@ -24,6 +24,7 @@ BANK_SCORE = [0, 1]
 BANK_WEIGHTS = [[4, 5], [2, 3]]
 BANK_VALS = [6, 7, 2, 3]
 BANK_SUM = [0, 1, 6, 4]
+BANK_WARM = 5
 GUESS = 0.9375
 Y_SPLIT = 160
 AT_VALS = [8192 * r for r in range(4)]
@@ -199,6 +200,11 @@ def tile_attend_cascade_pl_kernel(tc, query, pkey, pval, keys_words, keys_scales
             quantize(codes[:], scales[:], values[:])
             return codes, scales
 
+        def warm_up(codes, scales, name):
+            bank = in_bank(BANK_WARM, [P, 512], name)
+            nc.tensor.matmul_mx(out=bank[:], lhsT=codes.bitcast(FP8X4), lhsT_scale=scales,
+                                rhs=pk[0][:].bitcast(FP8X4), rhs_scale=pk[1][:], start=True, stop=True)
+
         acc = []
 
         def open_sum(r, vt, xt):
@@ -232,17 +238,20 @@ def tile_attend_cascade_pl_kernel(tc, query, pkey, pval, keys_words, keys_scales
         vt01 = quantized(vt_bf01, 2 * P, "vt01", AT_VALS[2] + 2048)
         for r in range(2):
             open_sum(r, (vt01[0][:, r * P:(r + 1) * P], vt01[1][:, r * P:(r + 1) * P]), xt)
+        warm_up(vt01[0][:, :P], vt01[1][:, :P], "warm0")
         vt_bf2 = weave(nc.scalar.copy, 2, turned2)
         turned3 = gather_and_turn(3)
         wt = quantized(w_bf, Q, "wt", AT_VALS[3] + 1024)
-        open_sum(2, quantized(vt_bf2, P, "vt2", AT_VALS[3]), xt)
+        vt2 = quantized(vt_bf2, P, "vt2", AT_VALS[3])
+        open_sum(2, vt2, xt)
+        warm_up(vt2[0][:], vt2[1][:], "warm1")
 
         pv_src = [half[:].rearrange("p j (s r) -> p s j r", r=4) for half in pv_raw]
         pv_bf = alloc([P, 4, P, 4], BF16, "pv_bf")
         pv_dst = pv_bf[:].rearrange("p r s j -> p s j r")
         nc.scalar.copy(pv_dst[:, :P // 2], pv_src[0])
-        nc.scalar.copy(pv_dst[:, P // 2:, :, 0:2], pv_src[1][:, :, :, 0:2])
-        nc.vector.tensor_copy(pv_dst[:, P // 2:, :, 2:4], pv_src[1][:, :, :, 2:4])
+        nc.vector.tensor_copy(pv_dst[:, P // 2:, :, 0:2], pv_src[1][:, :, :, 0:2])
+        nc.scalar.copy(pv_dst[:, P // 2:, :, 2:4], pv_src[1][:, :, :, 2:4])
         vt_bf3 = weave(nc.scalar.copy, 3, turned3, AT_PVAL + 4096)
 
         y = alloc([P, 4, Q], F32, "y")

@@ -20,11 +20,12 @@ ACT = mybir.ActivationFunctionType
 P = 128
 PREFIX, SUFFIX = 0, 1
 PK_SPLIT = 336
-BANK_SCORE = [0, 1]
-BANK_WEIGHTS = [[4, 5], [2, 3]]
-BANK_VALS = [6, 7, 2, 3]
-BANK_SUM = [0, 1, 6, 4]
-BANK_WARM = 5
+BANK_SCORE = [[0, 1], [2, 3]]
+BANK_WEIGHTS = [[2, 3], [4, 5]]
+BANK_VALS = [4, 5, 0, 1]
+BANK_SUM = [6, 7, 2, 3]
+BANK_WARM = 4
+PV_SPLIT = 40
 GUESS = 0.9375
 Y_SPLIT = 160
 AT_VALS = [8192 * r for r in range(4)]
@@ -53,20 +54,17 @@ def tile_attend_cascade_pl_kernel(tc, query, pkey, pval, keys_words, keys_scales
         def quantize(codes, scales, values):
             nc.vector.quantize_mx(out=codes.bitcast(FP8X4), scales=scales, in_=values)
 
-        offsets = sb.tile([P, I // 16], U16, name="offsets")
-        nc.sync.dma_start(offsets[:], offs)
+        q_raw = alloc([P, 4, Q], F32, "q_raw")
+        nc.sync.dma_start(q_raw[:], query.rearrange("(p j) q -> p j q", j=4))
         lse = [alloc([P, 2], F32, "lse_prefix"), alloc([P, 2], F32, "lse_suffix")]
         nc.scalar.dma_start(lse[PREFIX][:], l1.rearrange("(p c) o -> p (c o)", c=2))
         nc.scalar.dma_start(lse[SUFFIX][:], l2.rearrange("(p c) o -> p (c o)", c=2))
+        offsets = sb.tile([P, I // 16], U16, name="offsets")
+        nc.sync.dma_start(offsets[:], offs)
         token_w = [alloc([P, 4], F32, "psz_cols"), alloc([P, 4], F32, "size_cols")]
-        key_words = alloc([P, T], U16, "key_words")
-        nc.sync.dma_start(key_words[:].bitcast(I32), keys_words[0].bitcast(I32))
-        q_raw = alloc([P, 4, Q], F32, "q_raw")
-        nc.sync.dma_start(q_raw[:], query.rearrange("(p j) q -> p j q", j=4))
         key_scales = alloc([P, T], U8, "key_scales", AT_KEY_SCALES)
         nc.vector.memset(key_scales[:].bitcast(I32), 0)
-        for quad in range(4):
-            nc.sync.dma_start(key_scales[quad:P:32, :].bitcast(I32), keys_scales[0, quad:16:4, :].bitcast(I32))
+        nc.sync.dma_start(key_scales[0:P:8, :].bitcast(I32), keys_scales[0].bitcast(I32))
         vals_by_r = vals.rearrange("(p r) t -> r p t", r=4)
 
         def load_vals(r):
@@ -76,16 +74,21 @@ def tile_attend_cascade_pl_kernel(tc, query, pkey, pval, keys_words, keys_scales
 
         pk_raw = alloc([P, 4, M], F32, "pk_raw", AT_PKEY)
         nc.sync.dma_start(pk_raw[:], pkey.rearrange("(p j) m -> p j m", j=4))
+        key_words = alloc([P, T], U16, "key_words")
+        nc.sync.dma_start(key_words[:].bitcast(I32), keys_words[0].bitcast(I32))
         val_pool = [load_vals(0)]
-        nc.sync.dma_start(token_w[SUFFIX][:], size.rearrange("o (p t) -> p (o t)", t=4))
-        val_pool.append(load_vals(1))
         nc.sync.dma_start(token_w[PREFIX][:], psz.rearrange("o (p t) -> p (o t)", t=4))
+        kg_rows = alloc([P, I], U8, "kg_rows")
+        nc.vector.tensor_copy(kg_rows[:], key_scales[:].indirect(offsets[:]))
+        kg_scales = alloc([P, I], U8, "kg_scales")
+        nc.vector.tensor_copy(kg_scales[:].bitcast(I32), kg_rows[:].bitcast(I32))
+        for j in range(1, 4):
+            nc.sync.dma_start(kg_scales[j:P:32, :].bitcast(I32), kg_rows[8 * j:P:32, :].bitcast(I32))
+        val_pool.append(load_vals(1))
+        nc.sync.dma_start(token_w[SUFFIX][:], size.rearrange("o (p t) -> p (o t)", t=4))
         val_pool.extend([load_vals(r) for r in range(2, 4)])
-        pv_raw = []
-        for h in range(2):
-            half = alloc([P, 4, E // 2], F32, "pv_raw%d" % h, AT_PVAL + 4096 * h)
-            nc.sync.dma_start(half[:], pval.rearrange("(p j) e -> p j e", j=4)[:, :, h * E // 2:(h + 1) * E // 2])
-            pv_raw.append(half)
+        pv_raw = alloc([P, 4, E], F32, "pv_raw", AT_PVAL)
+        nc.sync.dma_start(pv_raw[:], pval.rearrange("(p j) e -> p j e", j=4))
         ident = alloc([P, P], F32, "ident")
         make_identity(nc, ident[:])
 
@@ -115,21 +118,17 @@ def tile_attend_cascade_pl_kernel(tc, query, pkey, pval, keys_words, keys_scales
             nc.scalar.activation(neg_lse[:, c:c + 1], back1[:, c:c + 1], ACT.Identity,
                                  scale=slope[:, c:c + 1], bias=keep1[:, c:c + 1])
 
-        kg_words = alloc([P, I], U16, "kg_words")
-        nc.vector.tensor_copy(kg_words[:], key_words[:].indirect(offsets[:]))
-        kg_scales = alloc([P, I], U8, "kg_scales")
-        nc.vector.tensor_copy(kg_scales[:], key_scales[:].indirect(offsets[:]))
 
         q_bf = alloc([P, 4 * Q], BF16, "q_bf")
         nc.scalar.copy(
             q_bf[:].rearrange("p (c a b j) -> p a j b c", c=2, b=2, j=4),
             q_raw[:].rearrange("p j (a b c) -> p a j b c", b=2, c=2))
-        q_codes = alloc([P, Q], U32, "q_codes", AT_KEY_SCALES)
+        q_codes = alloc([P, Q], U32, "q_codes")
         q_scales = alloc([P, Q], U8, "q_scales")
         quantize(q_codes[:], q_scales[:], q_bf[:])
 
         def scores_exp(part, c, rhs, rhs_scale, at=None):
-            bank = in_bank(BANK_SCORE[c], [P, 512], "score%d%d" % (part, c))
+            bank = in_bank(BANK_SCORE[part][c], [P, 512], "score%d%d" % (part, c))
             nc.tensor.matmul_mx(out=bank[:], lhsT=q_codes[:, c * P:(c + 1) * P].bitcast(FP8X4),
                                 lhsT_scale=q_scales[:, c * P:(c + 1) * P], rhs=rhs, rhs_scale=rhs_scale,
                                 start=True, stop=True)
@@ -154,9 +153,8 @@ def tile_attend_cascade_pl_kernel(tc, query, pkey, pval, keys_words, keys_scales
 
         def merge(part, pairs, at=None):
             w_bf = alloc([P, 4 * Q], BF16, "w_bf%d" % part, at)
-            nc.vector.tensor_copy(w_bf[:].bitcast(F32).rearrange("p (q u) -> p q u", u=2),
-                                  pairs[:].rearrange("p u q e -> p (u q e)").bitcast(F32).rearrange(
-                                      "p (u q) -> p q u", u=2))
+            nc.scalar.copy(w_bf[:].bitcast(F32).rearrange("p (q u) -> p q u", u=2),
+                           pairs[:].rearrange("p u q e -> p (u q e)").bitcast(F32).rearrange("p (u q) -> p q u", u=2))
             return w_bf
 
         def turn_rows(part, c, ex):
@@ -222,19 +220,20 @@ def tile_attend_cascade_pl_kernel(tc, query, pkey, pval, keys_words, keys_scales
         pk_src = pk_raw[:].rearrange("p j (a i) -> p a j i", i=4)
         nc.vector.tensor_copy(pk_dst[:, :PK_SPLIT // 4, :, :], pk_src[:, :PK_SPLIT // 4, :, :])
         nc.scalar.copy(pk_dst[:, PK_SPLIT // 4:, :, :], pk_src[:, PK_SPLIT // 4:, :, :])
-        ex_suffix = [scores_exp(SUFFIX, c, kg_words[:].bitcast(FP4X4), kg_scales[:], AT_PKEY + 2048 * c)
-                     for c in range(2)]
-        turned_suffix = [turn_rows(SUFFIX, c, ex_suffix[c]) for c in range(2)]
         pk = quantized(pk_bf, M, "pk")
+        kg_words = alloc([P, I], U16, "kg_words")
+        nc.vector.tensor_copy(kg_words[:], key_words[:].indirect(offsets[:]))
         ex_prefix = [scores_exp(PREFIX, c, pk[0][:].bitcast(FP8X4), pk[1][:]) for c in range(2)]
+        ex_suffix = [scores_exp(SUFFIX, c, kg_words[:].bitcast(FP4X4), kg_scales[:]) for c in range(2)]
+        turned_suffix = [turn_rows(SUFFIX, c, ex_suffix[c]) for c in range(2)]
+        w_pairs = turn_and_weigh(PREFIX, ex_prefix)
         vt_bf01 = alloc([P, 8 * P], BF16, "vt_bf01")
         weave(nc.scalar.copy, 0, gather_and_turn(0), None, vt_bf01[:, :4 * P])
-        xt = weigh_on_vector(SUFFIX, turned_suffix)
         turned1 = gather_and_turn(1)
-        w_pairs = turn_and_weigh(PREFIX, ex_prefix, AT_EX)
+        xt = weigh_on_vector(SUFFIX, turned_suffix)
         weave(nc.scalar.copy, 1, turned1, None, vt_bf01[:, 4 * P:])
+        w_bf = merge(PREFIX, w_pairs)
         turned2 = gather_and_turn(2)
-        w_bf = merge(PREFIX, w_pairs, AT_VALS[2])
         vt01 = quantized(vt_bf01, 2 * P, "vt01", AT_VALS[2] + 2048)
         for r in range(2):
             open_sum(r, (vt01[0][:, r * P:(r + 1) * P], vt01[1][:, r * P:(r + 1) * P]), xt)
@@ -246,18 +245,18 @@ def tile_attend_cascade_pl_kernel(tc, query, pkey, pval, keys_words, keys_scales
         open_sum(2, vt2, xt)
         warm_up(vt2[0][:], vt2[1][:], "warm1")
 
-        pv_src = [half[:].rearrange("p j (s r) -> p s j r", r=4) for half in pv_raw]
-        pv_bf = alloc([P, 4, P, 4], BF16, "pv_bf")
-        pv_dst = pv_bf[:].rearrange("p r s j -> p s j r")
-        nc.scalar.copy(pv_dst[:, :P // 2], pv_src[0])
-        nc.vector.tensor_copy(pv_dst[:, P // 2:, :, 0:2], pv_src[1][:, :, :, 0:2])
-        nc.scalar.copy(pv_dst[:, P // 2:, :, 2:4], pv_src[1][:, :, :, 2:4])
-        vt_bf3 = weave(nc.scalar.copy, 3, turned3, AT_PVAL + 4096)
+        pv_src = pv_raw[:].rearrange("p j (s r) -> p s j r", r=4)
+        pv_bf = [alloc([P, 2, P, 4], BF16, "pv_bf%d" % h) for h in range(2)]
+        pv_dst = [t[:].rearrange("p r s j -> p s j r") for t in pv_bf]
+        nc.scalar.copy(pv_dst[1][:, PV_SPLIT:], pv_src[:, PV_SPLIT:, :, 2:4])
+        nc.vector.tensor_copy(pv_dst[0], pv_src[:, :, :, 0:2])
+        nc.vector.tensor_copy(pv_dst[1][:, :PV_SPLIT], pv_src[:, :PV_SPLIT, :, 2:4])
+        vt_bf3 = weave(nc.scalar.copy, 3, turned3, AT_PVAL)
 
         y = alloc([P, 4, Q], F32, "y")
         out_by_r = out_0.rearrange("(p r) q -> p r q", r=4)
         def pv_operand(r):
-            return quantized(pv_bf[:, r, :, :].rearrange("p s j -> p (s j)"), P, "pv%d" % r)
+            return quantized(pv_bf[r // 2][:, r % 2, :, :].rearrange("p s j -> p (s j)"), P, "pv%d" % r)
 
         close_sum(0, pv_operand(0), wt)
         close_sum(1, pv_operand(1), wt)

@@ -54,6 +54,7 @@ def tile_attend_cascade_pl_kernel(tc, query, pkey, pval, keys_words, keys_scales
         def quantize(codes, scales, values):
             nc.vector.quantize_mx(out=codes.bitcast(FP8X4), scales=scales, in_=values)
 
+
         q_raw = alloc([P, 4, Q], F32, "q_raw")
         nc.sync.dma_start(q_raw[:], query.rearrange("(p j) q -> p j q", j=4))
         lse = [alloc([P, 2], F32, "lse_prefix"), alloc([P, 2], F32, "lse_suffix")]
@@ -170,6 +171,10 @@ def tile_attend_cascade_pl_kernel(tc, query, pkey, pval, keys_words, keys_scales
                 nc.vector.tensor_tensor(half[:], bank[:].rearrange("p t s -> p s t"),
                                         token_w[part][:].unsqueeze(1).to_broadcast([P, P, 4]), ALU.mult)
                 halves.append(half)
+                if c == 0:
+                    pass
+                if c == 1:
+                    pass
             codes = alloc([P, Q], U32, "w_codes%d" % part)
             scales = alloc([P, Q], U8, "w_scales%d" % part)
             for c in range(2):
@@ -180,6 +185,14 @@ def tile_attend_cascade_pl_kernel(tc, query, pkey, pval, keys_words, keys_scales
         def gather_and_turn(r):
             picked = alloc([P, I], BF16, "picked%d" % r)
             nc.vector.tensor_copy(picked[:], val_pool[r][:].indirect(offsets[:]))
+            if r == 0:
+                pass
+            if r == 1:
+                pass
+            if r == 2:
+                pass
+            if r == 3:
+                pass
             pairs = picked[:].bitcast(F32)
             bank = in_bank(BANK_VALS[r], [P, 2, P], "turned_vals%d" % r)
             for u in range(2):
@@ -241,9 +254,9 @@ def tile_attend_cascade_pl_kernel(tc, query, pkey, pval, keys_words, keys_scales
         vt_bf2 = weave(nc.scalar.copy, 2, turned2)
         turned3 = gather_and_turn(3)
         wt = quantized(w_bf, Q, "wt", AT_VALS[3] + 1024)
+        warm_up(wt[0][:, :P], wt[1][:, :P], "warm1")
         vt2 = quantized(vt_bf2, P, "vt2", AT_VALS[3])
         open_sum(2, vt2, xt)
-        warm_up(vt2[0][:], vt2[1][:], "warm1")
 
         pv_src = pv_raw[:].rearrange("p j (s r) -> p s j r", r=4)
         pv_bf = [alloc([P, 2, P, 4], BF16, "pv_bf%d" % h) for h in range(2)]

@@ -18,12 +18,14 @@ ALU = mybir.AluOpType
 ACT = mybir.ActivationFunctionType
 
 P = 128
+H = P // 2
 PREFIX, SUFFIX = 0, 1
 PK_SPLIT = 336
 BANK_SCORE = [[0, 1], [2, 3]]
 BANK_WEIGHTS = [[2, 3], [4, 5]]
 BANK_VALS = [4, 5, 0, 1]
-BANK_SUM = [6, 7, 2, 3]
+BANK_SUM = [6, 7, 2]
+BANK_LAST = [3, 5]
 BANK_WARM = 4
 PV_SPLIT = 40
 GUESS = 0.9375
@@ -99,20 +101,19 @@ def tile_attend_cascade_pl_kernel(tc, query, pkey, pval, keys_words, keys_scales
         top, low, below, rest = small("top"), small("low"), small("below"), small("rest")
         nc.vector.tensor_tensor(top[:], lse[PREFIX][:], lse[SUFFIX][:], ALU.max)
         nc.vector.tensor_tensor(low[:], lse[PREFIX][:], lse[SUFFIX][:], ALU.min)
-        nc.vector.tensor_scalar(rest[:], top[:], -1.0, 1.0, ALU.mult, ALU.add)
+        nc.vector.tensor_scalar(rest[:], top[:], -1.0, 2.0 - GUESS * GUESS, ALU.mult, ALU.add)
         nc.vector.tensor_sub(below[:], low[:], top[:])
         ratio, square, slope = small("ratio"), small("square"), small("slope")
         nc.scalar.activation(ratio[:], below[:], ACT.Exp)
         nc.scalar.activation(square[:], ratio[:], ACT.Square, scale=0.5, bias=-GUESS)
         nc.scalar.activation(slope[:], ratio[:], ACT.Identity, scale=-1.0, bias=-1.0)
-        back0, keep0, step1 = small("back0"), small("keep0"), small("step1")
+        back0, step1 = small("back0"), small("step1")
         nc.scalar.activation(back0[:], square[:], ACT.Exp, bias=-GUESS * GUESS)
-        nc.scalar.activation(keep0[:], square[:], ACT.Identity, bias=1.0 - GUESS * GUESS)
         for c in range(2):
             nc.scalar.activation(step1[:, c:c + 1], back0[:, c:c + 1], ACT.Identity,
-                                 scale=slope[:, c:c + 1], bias=keep0[:, c:c + 1])
+                                 scale=slope[:, c:c + 1], bias=square[:, c:c + 1])
         back1, keep1, neg_lse = small("back1"), small("keep1"), small("neg_lse")
-        nc.scalar.activation(back1[:], step1[:], ACT.Exp)
+        nc.scalar.activation(back1[:], step1[:], ACT.Exp, bias=1.0 - GUESS * GUESS)
         for c in range(2):
             nc.scalar.activation(keep1[:, c:c + 1], step1[:, c:c + 1], ACT.Identity, bias=rest[:, c:c + 1])
         for c in range(2):
@@ -154,8 +155,9 @@ def tile_attend_cascade_pl_kernel(tc, query, pkey, pval, keys_words, keys_scales
 
         def merge(part, pairs, at=None):
             w_bf = alloc([P, 4 * Q], BF16, "w_bf%d" % part, at)
-            nc.scalar.copy(w_bf[:].bitcast(F32).rearrange("p (q u) -> p q u", u=2),
-                           pairs[:].rearrange("p u q e -> p (u q e)").bitcast(F32).rearrange("p (u q) -> p q u", u=2))
+            nc.scalar.copy(w_bf[:].bitcast(F32).rearrange("p (h c s u) -> p h c s u", h=2, c=2, u=2),
+                           pairs[:].rearrange("p u q e -> p (u q e)").bitcast(F32).rearrange(
+                               "p (u c h s) -> p h c s u", u=2, c=2, h=2))
             return w_bf
 
         def turn_rows(part, c, ex):
@@ -165,22 +167,12 @@ def tile_attend_cascade_pl_kernel(tc, query, pkey, pval, keys_words, keys_scales
             return bank
 
         def weigh_on_vector(part, banks):
-            halves = []
+            x_bf = alloc([P, 4 * Q], BF16, "x_bf")
+            x_dst = x_bf[:].rearrange("p (h c s t) -> p c h s t", h=2, c=2, t=4)
             for c, bank in enumerate(banks):
-                half = alloc([P, P, 4], BF16, "w_half%d%d" % (part, c))
-                nc.vector.tensor_tensor(half[:], bank[:].rearrange("p t s -> p s t"),
-                                        token_w[part][:].unsqueeze(1).to_broadcast([P, P, 4]), ALU.mult)
-                halves.append(half)
-                if c == 0:
-                    pass
-                if c == 1:
-                    pass
-            codes = alloc([P, Q], U32, "w_codes%d" % part)
-            scales = alloc([P, Q], U8, "w_scales%d" % part)
-            for c in range(2):
-                quantize(codes[:, c * P:(c + 1) * P], scales[:, c * P:(c + 1) * P],
-                         halves[c][:].rearrange("p s t -> p (s t)"))
-            return codes, scales
+                nc.vector.tensor_tensor(x_dst[:, c], bank[:].rearrange("p t (h s) -> p h s t", h=2),
+                                        token_w[part][:].unsqueeze(1).unsqueeze(1).to_broadcast([P, 2, H, 4]), ALU.mult)
+            return x_bf
 
         def gather_and_turn(r):
             picked = alloc([P, I], BF16, "picked%d" % r)
@@ -243,10 +235,11 @@ def tile_attend_cascade_pl_kernel(tc, query, pkey, pval, keys_words, keys_scales
         vt_bf01 = alloc([P, 8 * P], BF16, "vt_bf01")
         weave(nc.scalar.copy, 0, gather_and_turn(0), None, vt_bf01[:, :4 * P])
         turned1 = gather_and_turn(1)
-        xt = weigh_on_vector(SUFFIX, turned_suffix)
+        x_bf = weigh_on_vector(SUFFIX, turned_suffix)
         weave(nc.scalar.copy, 1, turned1, None, vt_bf01[:, 4 * P:])
         w_bf = merge(PREFIX, w_pairs)
         turned2 = gather_and_turn(2)
+        xt = quantized(x_bf, Q, "xt", AT_VALS[2])
         vt01 = quantized(vt_bf01, 2 * P, "vt01", AT_VALS[2] + 2048)
         for r in range(2):
             open_sum(r, (vt01[0][:, r * P:(r + 1) * P], vt01[1][:, r * P:(r + 1) * P]), xt)
@@ -274,20 +267,37 @@ def tile_attend_cascade_pl_kernel(tc, query, pkey, pval, keys_words, keys_scales
         close_sum(0, pv_operand(0), wt)
         close_sum(1, pv_operand(1), wt)
         close_sum(2, pv_operand(2), wt)
-        open_sum(3, pv_operand(3), wt)
-        close_sum(3, quantized(vt_bf3, P, "vt3"), xt)
-        for r in range(4):
+        last = [in_bank(BANK_LAST[h], [P, P], "last%d" % h) for h in range(2)]
+
+        def last_passes(values, weights, opens):
+            for h in range(2):
+                cols = slice(h * P, (h + 1) * P)
+                nc.tensor.matmul_mx(out=last[h][:], lhsT=values[0][:].bitcast(FP8X4), lhsT_scale=values[1][:],
+                                    rhs=weights[0][:, cols].bitcast(FP8X4), rhs_scale=weights[1][:, cols],
+                                    start=opens, stop=not opens)
+
+        last_passes(pv_operand(3), wt, True)
+        last_passes(quantized(vt_bf3, P, "vt3"), xt, False)
+        for r in range(3):
             copy = nc.vector.tensor_copy if r == 2 else nc.scalar.copy
-            copy(y[:, r, :].rearrange("p (s c) -> p s c", c=2), acc[r][:].rearrange("p (c s) -> p s c", c=2))
-            if r % 2 == 1:
-                nc.sync.dma_start(out_by_r[:, r - 1:r + 1, :], y[:, r - 1:r + 1, :])
+            copy(y[:, r, :].rearrange("p (h s c) -> p h s c", h=2, c=2), acc[r][:].rearrange("p (h c s) -> p h s c", h=2, c=2))
+        nc.sync.dma_start(out_by_r[:, 0:3, :], y[:, 0:3, :])
 
         y_bf = alloc([P, 4 * Q], BF16, "y_bf")
-        y_dst = y_bf[:].rearrange("p (a i r) -> p a r i", i=4, r=4)
-        y_src = y[:].rearrange("p r (a i) -> p a r i", i=4)
-        nc.vector.tensor_copy(y_dst[:, :Y_SPLIT // 4, :, :], y_src[:, :Y_SPLIT // 4, :, :])
-        nc.scalar.copy(y_dst[:, Y_SPLIT // 4:, :, :], y_src[:, Y_SPLIT // 4:, :, :])
-        y_codes, y_scales = quantized(y_bf, Q, "y")
+        y_dst = y_bf[:].rearrange("p (h s c r) -> p h s c r", h=2, c=2, r=4)
+        y_src = y[:].rearrange("p r (h s c) -> p h s c r", h=2, c=2)
+        last_sums = [bank[:].rearrange("p (c s) -> p s c", c=2) for bank in last]
+        copies = (nc.vector.tensor_copy, nc.scalar.copy)
+        for h in range(2):
+            copies[h](y_dst[:, h, :, :, 0:3], y_src[:, h, :, :, 0:3])
+            copies[h](y_src[:, h, :, :, 3], last_sums[h])
+            copies[h](y_dst[:, h, :, :, 3], last_sums[h])
+        nc.sync.dma_start(out_by_r[:, 3, :], y[:, 3, :])
+        y_codes = alloc([P, Q], U32, "y_codes")
+        y_scales = alloc([P, Q], U8, "y_scales")
+        for h in (1, 0):
+            cols = slice(h * P, (h + 1) * P)
+            quantize(y_codes[:, cols], y_scales[:, cols], y_bf[:, 4 * h * P:4 * (h + 1) * P])
         nc.sync.dma_start(out_1[0].rearrange("p c r -> p (c r)").bitcast(I32), y_codes[:].bitcast(I32))
         for quad in range(4):
             queue = nc.scalar if quad % 2 == 0 else nc.sync

@@ -26,7 +26,6 @@ BANK_WEIGHTS = [[2, 3], [4, 5]]
 BANK_VALS = [4, 5, 0, 1]
 BANK_SUM = [6, 7, 2]
 BANK_LAST = [3, 5]
-BANK_WARM = 4
 PV_SPLIT = 40
 GUESS = 0.9375
 Y_SPLIT = 160
@@ -203,11 +202,6 @@ def tile_attend_cascade_pl_kernel(tc, query, pkey, pval, keys_words, keys_scales
             quantize(codes[:], scales[:], values[:])
             return codes, scales
 
-        def warm_up(codes, scales, name):
-            bank = in_bank(BANK_WARM, [P, 512], name)
-            nc.tensor.matmul_mx(out=bank[:], lhsT=codes.bitcast(FP8X4), lhsT_scale=scales,
-                                rhs=pk[0][:].bitcast(FP8X4), rhs_scale=pk[1][:], start=True, stop=True)
-
         acc = []
 
         def open_sum(r, vt, xt):
@@ -243,11 +237,9 @@ def tile_attend_cascade_pl_kernel(tc, query, pkey, pval, keys_words, keys_scales
         vt01 = quantized(vt_bf01, 2 * P, "vt01", AT_VALS[2] + 2048)
         for r in range(2):
             open_sum(r, (vt01[0][:, r * P:(r + 1) * P], vt01[1][:, r * P:(r + 1) * P]), xt)
-        warm_up(vt01[0][:, :P], vt01[1][:, :P], "warm0")
         vt_bf2 = weave(nc.scalar.copy, 2, turned2)
         turned3 = gather_and_turn(3)
         wt = quantized(w_bf, Q, "wt", AT_VALS[3] + 1024)
-        warm_up(wt[0][:, :P], wt[1][:, :P], "warm1")
         vt2 = quantized(vt_bf2, P, "vt2", AT_VALS[3])
         open_sum(2, vt2, xt)
 

@@ -21,23 +21,21 @@ P = 128
 H = P // 2
 PREFIX, SUFFIX = 0, 1
 PK_SPLIT = 336
-BANK_SCORE = [[0, 1], [2, 3]]
-BANK_WEIGHTS = [[2, 3], [4, 5]]
-BANK_VALS = [4, 5, 0, 1]
-BANK_SUM = [6, 7, 2]
-BANK_LAST = [3, 5]
 PV_SPLIT = 40
+LAST_GATHER_SPLIT = 18
 GUESS = 0.9375
-Y_SPLIT = 160
-AT_VALS = [8192 * r for r in range(4)]
-AT_PKEY = 4 * 8192
-AT_PVAL = 5 * 8192
-AT_KEY_SCALES = 6 * 8192
-AT_EX = 6 * 8192 + 2048
+BANK_SCORE = [[0, 1], [2, 3]]
+BANK_WEIGHTS = [[4, 5], [0, 1]]
+BANK_VALS = [2, 6, 7]
+BANK_SUMS01, BANK_SUM2 = 6, 4
+BANK_LAST = [6, 4]
+AT_WINDOW = [None, None, 24576, 0]
+AT_PKEY = 8192
+AT_PVAL = 16384
 
 
 def tile_attend_cascade_pl_kernel(tc, query, pkey, pval, keys_words, keys_scales, vals, l1, l2, psz, size, offs,
-                                   out_0, out_1, out_2):
+                                       out_0, out_1, out_2):
     nc = tc.nc
     with ExitStack() as ctx:
         sb = ctx.enter_context(tc.tile_pool(name="sb", bufs=1))
@@ -52,9 +50,18 @@ def tile_attend_cascade_pl_kernel(tc, query, pkey, pval, keys_words, keys_scales
                 return sb.tile(shape, dtype, name=name, align_bytes=64)
             return reused.tile(shape, dtype, name=name, align_bytes=64, offset=at)
 
-        def quantize(codes, scales, values):
-            nc.vector.quantize_mx(out=codes.bitcast(FP8X4), scales=scales, in_=values)
+        def quantized(values, width, name, at=None):
+            codes = alloc([P, width], U32, name + "_codes", at)
+            scales = alloc([P, width], U8, name + "_scales")
+            nc.vector.quantize_mx(out=codes[:].bitcast(FP8X4), scales=scales[:], in_=values)
+            return codes, scales
 
+        def columns(operand, first, count):
+            return operand[0][:, first:first + count], operand[1][:, first:first + count]
+
+        def mx_pass(out, stationary, moving, start, stop, moving_dtype=FP8X4):
+            nc.tensor.matmul_mx(out=out, lhsT=stationary[0].bitcast(FP8X4), lhsT_scale=stationary[1],
+                                rhs=moving[0].bitcast(moving_dtype), rhs_scale=moving[1], start=start, stop=stop)
 
         q_raw = alloc([P, 4, Q], F32, "q_raw")
         nc.sync.dma_start(q_raw[:], query.rearrange("(p j) q -> p j q", j=4))
@@ -64,21 +71,21 @@ def tile_attend_cascade_pl_kernel(tc, query, pkey, pval, keys_words, keys_scales
         offsets = sb.tile([P, I // 16], U16, name="offsets")
         nc.sync.dma_start(offsets[:], offs)
         token_w = [alloc([P, 4], F32, "psz_cols"), alloc([P, 4], F32, "size_cols")]
-        key_scales = alloc([P, T], U8, "key_scales", AT_KEY_SCALES)
+        key_scales = alloc([P, T], U8, "key_scales")
         nc.vector.memset(key_scales[:].bitcast(I32), 0)
         nc.sync.dma_start(key_scales[0:P:8, :].bitcast(I32), keys_scales[0].bitcast(I32))
         vals_by_r = vals.rearrange("(p r) t -> r p t", r=4)
 
-        def load_vals(r):
-            pool_r = alloc([P, T], F32, "val_pool%d" % r, AT_VALS[r])
-            nc.sync.dma_start(pool_r[:], vals_by_r[r])
-            return pool_r
+        def load_window(r):
+            window = alloc([P, T], F32, "window%d" % r, AT_WINDOW[r])
+            nc.sync.dma_start(window[:], vals_by_r[r])
+            return window
 
         pk_raw = alloc([P, 4, M], F32, "pk_raw", AT_PKEY)
         nc.sync.dma_start(pk_raw[:], pkey.rearrange("(p j) m -> p j m", j=4))
         key_words = alloc([P, T], U16, "key_words")
         nc.sync.dma_start(key_words[:].bitcast(I32), keys_words[0].bitcast(I32))
-        val_pool = [load_vals(0)]
+        windows = [load_window(0)]
         nc.sync.dma_start(token_w[PREFIX][:], psz.rearrange("o (p t) -> p (o t)", t=4))
         kg_rows = alloc([P, I], U8, "kg_rows")
         nc.vector.tensor_copy(kg_rows[:], key_scales[:].indirect(offsets[:]))
@@ -86,78 +93,47 @@ def tile_attend_cascade_pl_kernel(tc, query, pkey, pval, keys_words, keys_scales
         nc.vector.tensor_copy(kg_scales[:].bitcast(I32), kg_rows[:].bitcast(I32))
         for j in range(1, 4):
             nc.sync.dma_start(kg_scales[j:P:32, :].bitcast(I32), kg_rows[8 * j:P:32, :].bitcast(I32))
-        val_pool.append(load_vals(1))
+        windows.append(load_window(1))
         nc.sync.dma_start(token_w[SUFFIX][:], size.rearrange("o (p t) -> p (o t)", t=4))
-        val_pool.extend([load_vals(r) for r in range(2, 4)])
+        windows.append(load_window(2))
         pv_raw = alloc([P, 4, E], F32, "pv_raw", AT_PVAL)
         nc.sync.dma_start(pv_raw[:], pval.rearrange("(p j) e -> p j e", j=4))
+        windows.append(load_window(3))
         ident = alloc([P, P], F32, "ident")
         make_identity(nc, ident[:])
 
-        def small(name):
-            return alloc([P, 2], F32, name)
+        def small(name, at=None):
+            return alloc([P, 2], F32, name, at)
 
-        top, low, below, rest = small("top"), small("low"), small("below"), small("rest")
-        nc.vector.tensor_tensor(top[:], lse[PREFIX][:], lse[SUFFIX][:], ALU.max)
-        nc.vector.tensor_tensor(low[:], lse[PREFIX][:], lse[SUFFIX][:], ALU.min)
-        nc.vector.tensor_scalar(rest[:], top[:], -1.0, 2.0 - GUESS * GUESS, ALU.mult, ALU.add)
-        nc.vector.tensor_sub(below[:], low[:], top[:])
-        ratio, square, slope = small("ratio"), small("square"), small("slope")
-        nc.scalar.activation(ratio[:], below[:], ACT.Exp)
-        nc.scalar.activation(square[:], ratio[:], ACT.Square, scale=0.5, bias=-GUESS)
+        neg_l1, apart, ratio, slope = small("neg_l1"), small("apart"), small("ratio"), small("slope")
+        nc.scalar.activation(neg_l1[:], lse[PREFIX][:], ACT.Identity, scale=-1.0)
+        for c in range(2):
+            nc.scalar.activation(apart[:, c:c + 1], lse[SUFFIX][:, c:c + 1], ACT.Abs, bias=neg_l1[:, c:c + 1])
+        nc.scalar.activation(ratio[:], apart[:], ACT.Exp, scale=-1.0)
         nc.scalar.activation(slope[:], ratio[:], ACT.Identity, scale=-1.0, bias=-1.0)
-        back0, step1 = small("back0"), small("step1")
+        neg_top, square, back0, step1, keep1 = small("neg_top"), small("square"), small("back0"), small("step1"), small("keep1")
+        nc.vector.scalar_tensor_tensor(neg_top[:], lse[SUFFIX][:], -1.0, neg_l1[:], ALU.mult, ALU.min)
+        nc.scalar.activation(square[:], ratio[:], ACT.Square, scale=0.5, bias=-GUESS)
         nc.scalar.activation(back0[:], square[:], ACT.Exp, bias=-GUESS * GUESS)
         for c in range(2):
             nc.scalar.activation(step1[:, c:c + 1], back0[:, c:c + 1], ACT.Identity,
                                  scale=slope[:, c:c + 1], bias=square[:, c:c + 1])
-        back1, keep1, neg_lse = small("back1"), small("keep1"), small("neg_lse")
-        nc.scalar.activation(back1[:], step1[:], ACT.Exp, bias=1.0 - GUESS * GUESS)
-        for c in range(2):
-            nc.scalar.activation(keep1[:, c:c + 1], step1[:, c:c + 1], ACT.Identity, bias=rest[:, c:c + 1])
-        for c in range(2):
-            nc.scalar.activation(neg_lse[:, c:c + 1], back1[:, c:c + 1], ACT.Identity,
-                                 scale=slope[:, c:c + 1], bias=keep1[:, c:c + 1])
-
+        nc.vector.scalar_tensor_tensor(keep1[:], step1[:], 2.0 - GUESS * GUESS, neg_top[:], ALU.add, ALU.add)
 
         q_bf = alloc([P, 4 * Q], BF16, "q_bf")
         nc.scalar.copy(
             q_bf[:].rearrange("p (c a b j) -> p a j b c", c=2, b=2, j=4),
             q_raw[:].rearrange("p j (a b c) -> p a j b c", b=2, c=2))
-        q_codes = alloc([P, Q], U32, "q_codes")
-        q_scales = alloc([P, Q], U8, "q_scales")
-        quantize(q_codes[:], q_scales[:], q_bf[:])
+        qq = quantized(q_bf[:], Q, "q")
 
-        def scores_exp(part, c, rhs, rhs_scale, at=None):
+        def scores_exp(part, c, keys, keys_dtype):
             bank = in_bank(BANK_SCORE[part][c], [P, 512], "score%d%d" % (part, c))
-            nc.tensor.matmul_mx(out=bank[:], lhsT=q_codes[:, c * P:(c + 1) * P].bitcast(FP8X4),
-                                lhsT_scale=q_scales[:, c * P:(c + 1) * P], rhs=rhs, rhs_scale=rhs_scale,
-                                start=True, stop=True)
-            ex = alloc([P, 512], F32, "ex%d%d" % (part, c), at)
+            mx_pass(bank[:], columns(qq, c * P, P), keys, True, True, keys_dtype)
+            ex = alloc([P, 512], F32, "ex%d%d" % (part, c))
             nc.scalar.activation(ex[:].rearrange("q (t p) -> q t p", t=4),
                                  bank[:].rearrange("q (p t) -> q t p", t=4),
                                  ACT.Exp, bias=neg_lse[:, c:c + 1])
             return ex
-
-        def turn_and_weigh(part, ex, at=None):
-            pairs = alloc([P, 2, Q, 2], BF16, "pairs%d" % part, at)
-            for u in range(2):
-                bank = in_bank(BANK_WEIGHTS[part][u], [P, 2, Q], "turned%d%d" % (part, u))
-                for c in range(2):
-                    for e in range(2):
-                        t = 2 * u + e
-                        nc.tensor.transpose(bank[:, e, c * P:(c + 1) * P], ex[c][:, t * P:(t + 1) * P], ident[:])
-                for e in range(2):
-                    t = 2 * u + e
-                    nc.scalar.activation(pairs[:, u, :, e], bank[:, e, :], ACT.Copy, scale=token_w[part][:, t:t + 1])
-            return pairs
-
-        def merge(part, pairs, at=None):
-            w_bf = alloc([P, 4 * Q], BF16, "w_bf%d" % part, at)
-            nc.scalar.copy(w_bf[:].bitcast(F32).rearrange("p (h c s u) -> p h c s u", h=2, c=2, u=2),
-                           pairs[:].rearrange("p u q e -> p (u q e)").bitcast(F32).rearrange(
-                               "p (u c h s) -> p h c s u", u=2, c=2, h=2))
-            return w_bf
 
         def turn_rows(part, c, ex):
             bank = in_bank(BANK_WEIGHTS[part][c], [P, 4, P], "turned%d%d" % (part, c))
@@ -165,83 +141,67 @@ def tile_attend_cascade_pl_kernel(tc, query, pkey, pval, keys_words, keys_scales
                 nc.tensor.transpose(bank[:, t, :], ex[:, t * P:(t + 1) * P], ident[:])
             return bank
 
-        def weigh_on_vector(part, banks):
-            x_bf = alloc([P, 4 * Q], BF16, "x_bf")
-            x_dst = x_bf[:].rearrange("p (h c s t) -> p c h s t", h=2, c=2, t=4)
-            for c, bank in enumerate(banks):
-                nc.vector.tensor_tensor(x_dst[:, c], bank[:].rearrange("p t (h s) -> p h s t", h=2),
-                                        token_w[part][:].unsqueeze(1).unsqueeze(1).to_broadcast([P, 2, H, 4]), ALU.mult)
-            return x_bf
+        def weigh(part, c, bank, w_bf):
+            w_dst = w_bf[:].rearrange("p (h c s t) -> p c h s t", h=2, c=2, t=4)
+            nc.vector.tensor_tensor(w_dst[:, c], bank[:].rearrange("p t (h s) -> p h s t", h=2),
+                                    token_w[part][:].unsqueeze(1).unsqueeze(1).to_broadcast([P, 2, H, 4]), ALU.mult)
 
-        def gather_and_turn(r):
+        def gather(r, vector_columns):
             picked = alloc([P, I], BF16, "picked%d" % r)
-            nc.vector.tensor_copy(picked[:], val_pool[r][:].indirect(offsets[:]))
-            if r == 0:
-                pass
-            if r == 1:
-                pass
-            if r == 2:
-                pass
-            if r == 3:
-                pass
-            pairs = picked[:].bitcast(F32)
-            bank = in_bank(BANK_VALS[r], [P, 2, P], "turned_vals%d" % r)
+            cut = 16 * vector_columns
+            if cut > 0:
+                nc.vector.tensor_copy(picked[:, :cut], windows[r][:].indirect(offsets[:, :vector_columns]))
+            if cut < I:
+                nc.scalar.activation(picked[:, cut:], windows[r][:].indirect(offsets[:, vector_columns:]), ACT.Copy)
+            return [picked[:].bitcast(F32)[:, u:I // 2:2] for u in range(2)]
+
+        def gather_sorted(r):
+            picked = alloc([P, 2, P, 2], BF16, "picked%d" % r)
+            nc.vector.tensor_copy(picked[:].rearrange("p u s e -> p s u e"), windows[r][:].indirect(offsets[:]))
+            pairs = picked[:].rearrange("p u s e -> p u (s e)").bitcast(F32)
+            return [pairs[:, u, :] for u in range(2)]
+
+        def turn(pairs, bank):
             for u in range(2):
-                nc.tensor.transpose(bank[:, u, :], pairs[:, u:I // 2:2], ident[:])
-            return bank
+                nc.tensor.transpose(bank[:, u, :], pairs[u], ident[:])
 
-        def weave(copy, r, bank, at=None, vt_bf=None):
-            if vt_bf is None:
-                vt_bf = alloc([P, 4 * P], BF16, "vt_bf%d" % r, at)
-            copy(vt_bf[:].bitcast(F32).rearrange("p (s u) -> p s u", u=2), bank[:].rearrange("p u s -> p s u"))
-            return vt_bf
-
-        def quantized(values, width, name, slot=None):
-            codes = alloc([P, width], U32, name + "_codes", slot)
-            scales = alloc([P, width], U8, name + "_scales")
-            quantize(codes[:], scales[:], values[:])
-            return codes, scales
-
-        acc = []
-
-        def open_sum(r, vt, xt):
-            bank = in_bank(BANK_SUM[r], [P, Q], "sum%d" % r)
-            nc.tensor.matmul_mx(out=bank[:], lhsT=vt[0][:].bitcast(FP8X4), lhsT_scale=vt[1][:],
-                                rhs=xt[0][:].bitcast(FP8X4), rhs_scale=xt[1][:], start=True, stop=False)
-            acc.append(bank)
-
-        def close_sum(r, vt, xt):
-            nc.tensor.matmul_mx(out=acc[r][:], lhsT=vt[0][:].bitcast(FP8X4), lhsT_scale=vt[1][:],
-                                rhs=xt[0][:].bitcast(FP8X4), rhs_scale=xt[1][:], start=False, stop=True)
+        def weave(vt_bf, bank):
+            nc.scalar.copy(vt_bf.bitcast(F32).rearrange("p r (s u) -> p r s u", u=2), bank.rearrange("p r u s -> p r s u"))
 
         pk_bf = alloc([P, 4 * M], BF16, "pk_bf")
         pk_dst = pk_bf[:].rearrange("p (a i j) -> p a j i", i=4, j=4)
         pk_src = pk_raw[:].rearrange("p j (a i) -> p a j i", i=4)
         nc.vector.tensor_copy(pk_dst[:, :PK_SPLIT // 4, :, :], pk_src[:, :PK_SPLIT // 4, :, :])
         nc.scalar.copy(pk_dst[:, PK_SPLIT // 4:, :, :], pk_src[:, PK_SPLIT // 4:, :, :])
-        pk = quantized(pk_bf, M, "pk")
+        pk = quantized(pk_bf[:], M, "pk")
+        back1, neg_lse = small("back1", AT_PKEY), small("neg_lse")
+        nc.scalar.activation(back1[:], step1[:], ACT.Exp, bias=1.0 - GUESS * GUESS)
+        for c in range(2):
+            nc.scalar.activation(neg_lse[:, c:c + 1], back1[:, c:c + 1], ACT.Identity,
+                                 scale=slope[:, c:c + 1], bias=keep1[:, c:c + 1])
         kg_words = alloc([P, I], U16, "kg_words")
         nc.vector.tensor_copy(kg_words[:], key_words[:].indirect(offsets[:]))
-        ex_prefix = [scores_exp(PREFIX, c, pk[0][:].bitcast(FP8X4), pk[1][:]) for c in range(2)]
-        ex_suffix = [scores_exp(SUFFIX, c, kg_words[:].bitcast(FP4X4), kg_scales[:]) for c in range(2)]
-        turned_suffix = [turn_rows(SUFFIX, c, ex_suffix[c]) for c in range(2)]
-        w_pairs = turn_and_weigh(PREFIX, ex_prefix)
-        vt_bf01 = alloc([P, 8 * P], BF16, "vt_bf01")
-        weave(nc.scalar.copy, 0, gather_and_turn(0), None, vt_bf01[:, :4 * P])
-        turned1 = gather_and_turn(1)
-        x_bf = weigh_on_vector(SUFFIX, turned_suffix)
-        weave(nc.scalar.copy, 1, turned1, None, vt_bf01[:, 4 * P:])
-        w_bf = merge(PREFIX, w_pairs)
-        turned2 = gather_and_turn(2)
-        xt = quantized(x_bf, Q, "xt", AT_VALS[2])
-        vt01 = quantized(vt_bf01, 2 * P, "vt01", AT_VALS[2] + 2048)
-        for r in range(2):
-            open_sum(r, (vt01[0][:, r * P:(r + 1) * P], vt01[1][:, r * P:(r + 1) * P]), xt)
-        vt_bf2 = weave(nc.scalar.copy, 2, turned2)
-        turned3 = gather_and_turn(3)
-        wt = quantized(w_bf, Q, "wt", AT_VALS[3] + 1024)
-        vt2 = quantized(vt_bf2, P, "vt2", AT_VALS[3])
-        open_sum(2, vt2, xt)
+        ex_prefix = [scores_exp(PREFIX, c, columns(pk, 0, M), FP8X4) for c in range(2)]
+        picked0 = gather_sorted(0)
+        weights_bf = [alloc([P, 4 * Q], BF16, "weights%d" % part) for part in range(2)]
+        for c in range(2):
+            weigh(PREFIX, c, turn_rows(PREFIX, c, ex_prefix[c]), weights_bf[PREFIX])
+        wt = quantized(weights_bf[PREFIX][:], Q, "wt")
+        ex_suffix = [scores_exp(SUFFIX, c, (kg_words[:], kg_scales[:]), FP4X4) for c in range(2)]
+        picked1 = gather_sorted(1)
+        for c in range(2):
+            weigh(SUFFIX, c, turn_rows(SUFFIX, c, ex_suffix[c]), weights_bf[SUFFIX])
+        xt = quantized(weights_bf[SUFFIX][:], Q, "xt")
+
+        turned01 = in_bank(BANK_VALS[0], [P, 2, 2, P], "turned_vals01")
+        turn(picked0, turned01[:, 0])
+        turn(picked1, turned01[:, 1])
+        turned2 = in_bank(BANK_VALS[1], [P, 1, 2, P], "turned_vals2")
+        turn(gather(2, 0), turned2[:, 0])
+        vt_bf01 = alloc([P, 2, 4 * P], BF16, "vt_bf01", AT_WINDOW[2])
+        weave(vt_bf01[:], turned01[:])
+        vt_bf2 = alloc([P, 1, 4 * P], BF16, "vt_bf2")
+        weave(vt_bf2[:], turned2[:])
 
         pv_src = pv_raw[:].rearrange("p j (s r) -> p s j r", r=4)
         pv_bf = [alloc([P, 2, P, 4], BF16, "pv_bf%d" % h) for h in range(2)]
@@ -249,47 +209,55 @@ def tile_attend_cascade_pl_kernel(tc, query, pkey, pval, keys_words, keys_scales
         nc.scalar.copy(pv_dst[1][:, PV_SPLIT:], pv_src[:, PV_SPLIT:, :, 2:4])
         nc.vector.tensor_copy(pv_dst[0], pv_src[:, :, :, 0:2])
         nc.vector.tensor_copy(pv_dst[1][:, :PV_SPLIT], pv_src[:, :PV_SPLIT, :, 2:4])
-        vt_bf3 = weave(nc.scalar.copy, 3, turned3, AT_PVAL)
+        pv01 = quantized(pv_bf[0][:].rearrange("p r s j -> p (r s j)"), 2 * P, "pv01")
+        vt01 = quantized(vt_bf01[:].rearrange("p r w -> p (r w)"), 2 * P, "vt01", AT_PVAL)
+        pv23 = quantized(pv_bf[1][:].rearrange("p r s j -> p (r s j)"), 2 * P, "pv23")
+        vt2 = quantized(vt_bf2[:, 0, :], P, "vt2", AT_PVAL + 1024)
 
-        y = alloc([P, 4, Q], F32, "y")
+        sums01 = in_bank(BANK_SUMS01, [P, 2, Q], "sums01")
+        for r in range(2):
+            mx_pass(sums01[:, r, :], columns(pv01, r * P, P), columns(wt, 0, Q), r == 0, False)
+        for r in range(2):
+            mx_pass(sums01[:, r, :], columns(vt01, r * P, P), columns(xt, 0, Q), False, r == 1)
+        sum2 = in_bank(BANK_SUM2, [P, Q], "sum2")
+        mx_pass(sum2[:], columns(pv23, 0, P), columns(wt, 0, Q), True, False)
+        mx_pass(sum2[:], columns(vt2, 0, P), columns(xt, 0, Q), False, True)
+
+        turned3 = in_bank(BANK_VALS[2], [P, 1, 2, P], "turned_vals3")
+        turn(gather(3, LAST_GATHER_SPLIT), turned3[:, 0])
+        y = alloc([P, 4, Q], F32, "y", AT_WINDOW[3])
         out_by_r = out_0.rearrange("(p r) q -> p r q", r=4)
-        def pv_operand(r):
-            return quantized(pv_bf[r // 2][:, r % 2, :, :].rearrange("p s j -> p (s j)"), P, "pv%d" % r)
-
-        close_sum(0, pv_operand(0), wt)
-        close_sum(1, pv_operand(1), wt)
-        close_sum(2, pv_operand(2), wt)
-        last = [in_bank(BANK_LAST[h], [P, P], "last%d" % h) for h in range(2)]
-
-        def last_passes(values, weights, opens):
-            for h in range(2):
-                cols = slice(h * P, (h + 1) * P)
-                nc.tensor.matmul_mx(out=last[h][:], lhsT=values[0][:].bitcast(FP8X4), lhsT_scale=values[1][:],
-                                    rhs=weights[0][:, cols].bitcast(FP8X4), rhs_scale=weights[1][:, cols],
-                                    start=opens, stop=not opens)
-
-        last_passes(pv_operand(3), wt, True)
-        last_passes(quantized(vt_bf3, P, "vt3"), xt, False)
-        for r in range(3):
-            copy = nc.vector.tensor_copy if r == 2 else nc.scalar.copy
-            copy(y[:, r, :].rearrange("p (h s c) -> p h s c", h=2, c=2), acc[r][:].rearrange("p (h c s) -> p h s c", h=2, c=2))
+        nc.scalar.copy(y[:, 0:2, :].rearrange("p r (h s c) -> p r h s c", h=2, c=2),
+                       sums01[:].rearrange("p r (h c s) -> p r h s c", h=2, c=2))
+        nc.vector.tensor_copy(y[:, 2, :].rearrange("p (h s c) -> p h s c", h=2, c=2),
+                              sum2[:].rearrange("p (h c s) -> p h s c", h=2, c=2))
         nc.sync.dma_start(out_by_r[:, 0:3, :], y[:, 0:3, :])
-
+        last = [in_bank(BANK_LAST[h], [P, P], "last%d" % h) for h in range(2)]
+        for h in range(2):
+            mx_pass(last[h][:], columns(pv23, P, P), columns(wt, h * P, P), True, False)
         y_bf = alloc([P, 4 * Q], BF16, "y_bf")
         y_dst = y_bf[:].rearrange("p (h s c r) -> p h s c r", h=2, c=2, r=4)
         y_src = y[:].rearrange("p r (h s c) -> p h s c r", h=2, c=2)
+        nc.vector.tensor_copy(y_dst[:, 0, :, :, 0:3], y_src[:, 0, :, :, 0:3])
+
+        vt_bf3 = alloc([P, 1, 4 * P], BF16, "vt_bf3")
+        weave(vt_bf3[:], turned3[:])
+        nc.scalar.copy(y_dst[:, 1, :, :, 0:3], y_src[:, 1, :, :, 0:3])
+        vt3 = quantized(vt_bf3[:, 0, :], P, "vt3")
+        for h in range(2):
+            mx_pass(last[h][:], columns(vt3, 0, P), columns(xt, h * P, P), False, True)
         last_sums = [bank[:].rearrange("p (c s) -> p s c", c=2) for bank in last]
         copies = (nc.vector.tensor_copy, nc.scalar.copy)
         for h in range(2):
-            copies[h](y_dst[:, h, :, :, 0:3], y_src[:, h, :, :, 0:3])
-            copies[h](y_src[:, h, :, :, 3], last_sums[h])
             copies[h](y_dst[:, h, :, :, 3], last_sums[h])
+            copies[h](y_src[:, h, :, :, 3], last_sums[h])
         nc.sync.dma_start(out_by_r[:, 3, :], y[:, 3, :])
         y_codes = alloc([P, Q], U32, "y_codes")
         y_scales = alloc([P, Q], U8, "y_scales")
         for h in (1, 0):
             cols = slice(h * P, (h + 1) * P)
-            quantize(y_codes[:, cols], y_scales[:, cols], y_bf[:, 4 * h * P:4 * (h + 1) * P])
+            nc.vector.quantize_mx(out=y_codes[:, cols].bitcast(FP8X4), scales=y_scales[:, cols],
+                                  in_=y_bf[:, 4 * h * P:4 * (h + 1) * P])
         nc.sync.dma_start(out_1[0].rearrange("p c r -> p (c r)").bitcast(I32), y_codes[:].bitcast(I32))
         for quad in range(4):
             queue = nc.scalar if quad % 2 == 0 else nc.sync

@@ -18,19 +18,19 @@ ALU = mybir.AluOpType
 ACT = mybir.ActivationFunctionType
 
 P = 128
-H = P // 2
 PREFIX, SUFFIX = 0, 1
 PK_SPLIT = 336
 PV_SPLIT = 40
-LAST_GATHER_SPLIT = 18
+LAST_GATHER_SPLIT = 16
 GUESS = 0.9375
 BANK_SCORE = [[0, 1], [2, 3]]
 BANK_WEIGHTS = [[4, 5], [0, 1]]
 BANK_VALS = [2, 6, 7]
 BANK_SUMS01, BANK_SUM2 = 6, 4
 BANK_LAST = [6, 4]
+BANK_LSE = 7
 AT_WINDOW = [None, None, 24576, 0]
-AT_PKEY = 8192
+AT_APART, AT_PKEY = 8192, 49152
 AT_PVAL = 16384
 
 
@@ -65,15 +65,16 @@ def tile_attend_cascade_pl_kernel(tc, query, pkey, pval, keys_words, keys_scales
 
         q_raw = alloc([P, 4, Q], F32, "q_raw")
         nc.sync.dma_start(q_raw[:], query.rearrange("(p j) q -> p j q", j=4))
-        lse = [alloc([P, 2], F32, "lse_prefix"), alloc([P, 2], F32, "lse_suffix")]
-        nc.scalar.dma_start(lse[PREFIX][:], l1.rearrange("(p c) o -> p (c o)", c=2))
-        nc.scalar.dma_start(lse[SUFFIX][:], l2.rearrange("(p c) o -> p (c o)", c=2))
         offsets = sb.tile([P, I // 16], U16, name="offsets")
         nc.sync.dma_start(offsets[:], offs)
-        token_w = [alloc([P, 4], F32, "psz_cols"), alloc([P, 4], F32, "size_cols")]
         key_scales = alloc([P, T], U8, "key_scales")
         nc.vector.memset(key_scales[:].bitcast(I32), 0)
         nc.sync.dma_start(key_scales[0:P:8, :].bitcast(I32), keys_scales[0].bitcast(I32))
+        rows = alloc([P, P], F32, "rows")
+        nc.gpsimd.memset(rows[:], 0.0)
+        nc.sync.dma_start(rows[0:2, :], l1.rearrange("(c p) o -> c (p o)", c=2))
+        nc.sync.dma_start(rows[2:4, :], l2.rearrange("(c p) o -> c (p o)", c=2))
+        token_w = [alloc([P, 4], F32, "psz_cols"), alloc([P, 4], F32, "size_cols")]
         vals_by_r = vals.rearrange("(p r) t -> r p t", r=4)
 
         def load_window(r):
@@ -102,28 +103,33 @@ def tile_attend_cascade_pl_kernel(tc, query, pkey, pval, keys_words, keys_scales
         ident = alloc([P, P], F32, "ident")
         make_identity(nc, ident[:])
 
+        lse_bank = in_bank(BANK_LSE, [P, P], "lse_columns")
+        nc.tensor.transpose(lse_bank[:], rows[:], ident[:])
+        lse = [lse_bank[:, 0:2], lse_bank[:, 2:4]]
+
         def small(name, at=None):
             return alloc([P, 2], F32, name, at)
 
-        neg_l1, apart, ratio, slope = small("neg_l1"), small("apart"), small("ratio"), small("slope")
-        nc.scalar.activation(neg_l1[:], lse[PREFIX][:], ACT.Identity, scale=-1.0)
+        neg_l1, apart, ratio, slope = small("neg_l1"), small("apart", AT_APART), small("ratio"), small("slope")
+        nc.scalar.activation(neg_l1[:], lse[PREFIX], ACT.Identity, scale=-1.0)
         for c in range(2):
             nc.scalar.activation(apart[:, c:c + 1], lse[SUFFIX][:, c:c + 1], ACT.Abs, bias=neg_l1[:, c:c + 1])
         nc.scalar.activation(ratio[:], apart[:], ACT.Exp, scale=-1.0)
         nc.scalar.activation(slope[:], ratio[:], ACT.Identity, scale=-1.0, bias=-1.0)
         neg_top, square, back0, step1, keep1 = small("neg_top"), small("square"), small("back0"), small("step1"), small("keep1")
-        nc.vector.scalar_tensor_tensor(neg_top[:], lse[SUFFIX][:], -1.0, neg_l1[:], ALU.mult, ALU.min)
+        rest = small("rest")
+        nc.vector.scalar_tensor_tensor(neg_top[:], lse[SUFFIX], -1.0, neg_l1[:], ALU.mult, ALU.min)
+        nc.vector.tensor_scalar_add(rest[:], neg_top[:], 2.0 - GUESS * GUESS)
         nc.scalar.activation(square[:], ratio[:], ACT.Square, scale=0.5, bias=-GUESS)
         nc.scalar.activation(back0[:], square[:], ACT.Exp, bias=-GUESS * GUESS)
         for c in range(2):
             nc.scalar.activation(step1[:, c:c + 1], back0[:, c:c + 1], ACT.Identity,
                                  scale=slope[:, c:c + 1], bias=square[:, c:c + 1])
-        nc.vector.scalar_tensor_tensor(keep1[:], step1[:], 2.0 - GUESS * GUESS, neg_top[:], ALU.add, ALU.add)
+        for c in range(2):
+            nc.scalar.activation(keep1[:, c:c + 1], step1[:, c:c + 1], ACT.Identity, bias=rest[:, c:c + 1])
 
         q_bf = alloc([P, 4 * Q], BF16, "q_bf")
-        nc.scalar.copy(
-            q_bf[:].rearrange("p (c a b j) -> p a j b c", c=2, b=2, j=4),
-            q_raw[:].rearrange("p j (a b c) -> p a j b c", b=2, c=2))
+        nc.scalar.copy(q_bf[:].rearrange("p (a i j) -> p a j i", i=4, j=4), q_raw[:].rearrange("p j (a i) -> p a j i", i=4))
         qq = quantized(q_bf[:], Q, "q")
 
         def scores_exp(part, c, keys, keys_dtype):
@@ -142,9 +148,8 @@ def tile_attend_cascade_pl_kernel(tc, query, pkey, pval, keys_words, keys_scales
             return bank
 
         def weigh(part, c, bank, w_bf):
-            w_dst = w_bf[:].rearrange("p (h c s t) -> p c h s t", h=2, c=2, t=4)
-            nc.vector.tensor_tensor(w_dst[:, c], bank[:].rearrange("p t (h s) -> p h s t", h=2),
-                                    token_w[part][:].unsqueeze(1).unsqueeze(1).to_broadcast([P, 2, H, 4]), ALU.mult)
+            nc.vector.tensor_tensor(w_bf[:].rearrange("p (c s t) -> p c s t", c=2, t=4)[:, c], bank[:].rearrange("p t s -> p s t"),
+                                    token_w[part][:].unsqueeze(1).to_broadcast([P, P, 4]), ALU.mult)
 
         def gather(r, vector_columns):
             picked = alloc([P, I], BF16, "picked%d" % r)
@@ -168,30 +173,31 @@ def tile_attend_cascade_pl_kernel(tc, query, pkey, pval, keys_words, keys_scales
         def weave(vt_bf, bank):
             nc.scalar.copy(vt_bf.bitcast(F32).rearrange("p r (s u) -> p r s u", u=2), bank.rearrange("p r u s -> p r s u"))
 
-        pk_bf = alloc([P, 4 * M], BF16, "pk_bf")
+        pk_bf = alloc([P, 4 * M], BF16, "pk_bf", AT_APART)
         pk_dst = pk_bf[:].rearrange("p (a i j) -> p a j i", i=4, j=4)
         pk_src = pk_raw[:].rearrange("p j (a i) -> p a j i", i=4)
         nc.vector.tensor_copy(pk_dst[:, :PK_SPLIT // 4, :, :], pk_src[:, :PK_SPLIT // 4, :, :])
         nc.scalar.copy(pk_dst[:, PK_SPLIT // 4:, :, :], pk_src[:, PK_SPLIT // 4:, :, :])
         pk = quantized(pk_bf[:], M, "pk")
-        back1, neg_lse = small("back1", AT_PKEY), small("neg_lse")
+        back1, neg_lse = small("back1"), small("neg_lse")
         nc.scalar.activation(back1[:], step1[:], ACT.Exp, bias=1.0 - GUESS * GUESS)
         for c in range(2):
             nc.scalar.activation(neg_lse[:, c:c + 1], back1[:, c:c + 1], ACT.Identity,
                                  scale=slope[:, c:c + 1], bias=keep1[:, c:c + 1])
-        kg_words = alloc([P, I], U16, "kg_words")
+        kg_words = alloc([P, I], U16, "kg_words", AT_PKEY)
         nc.vector.tensor_copy(kg_words[:], key_words[:].indirect(offsets[:]))
         ex_prefix = [scores_exp(PREFIX, c, columns(pk, 0, M), FP8X4) for c in range(2)]
         picked0 = gather_sorted(0)
-        weights_bf = [alloc([P, 4 * Q], BF16, "weights%d" % part) for part in range(2)]
+        w_bf = alloc([P, 4 * Q], BF16, "w_bf")
         for c in range(2):
-            weigh(PREFIX, c, turn_rows(PREFIX, c, ex_prefix[c]), weights_bf[PREFIX])
-        wt = quantized(weights_bf[PREFIX][:], Q, "wt")
+            weigh(PREFIX, c, turn_rows(PREFIX, c, ex_prefix[c]), w_bf)
+        wt = quantized(w_bf[:], Q, "wt")
         ex_suffix = [scores_exp(SUFFIX, c, (kg_words[:], kg_scales[:]), FP4X4) for c in range(2)]
         picked1 = gather_sorted(1)
+        x_bf = alloc([P, 4 * Q], BF16, "x_bf")
         for c in range(2):
-            weigh(SUFFIX, c, turn_rows(SUFFIX, c, ex_suffix[c]), weights_bf[SUFFIX])
-        xt = quantized(weights_bf[SUFFIX][:], Q, "xt")
+            weigh(SUFFIX, c, turn_rows(SUFFIX, c, ex_suffix[c]), x_bf)
+        xt = quantized(x_bf[:], Q, "xt")
 
         turned01 = in_bank(BANK_VALS[0], [P, 2, 2, P], "turned_vals01")
         turn(picked0, turned01[:, 0])
@@ -227,30 +233,27 @@ def tile_attend_cascade_pl_kernel(tc, query, pkey, pval, keys_words, keys_scales
         turn(gather(3, LAST_GATHER_SPLIT), turned3[:, 0])
         y = alloc([P, 4, Q], F32, "y", AT_WINDOW[3])
         out_by_r = out_0.rearrange("(p r) q -> p r q", r=4)
-        nc.scalar.copy(y[:, 0:2, :].rearrange("p r (h s c) -> p r h s c", h=2, c=2),
-                       sums01[:].rearrange("p r (h c s) -> p r h s c", h=2, c=2))
-        nc.vector.tensor_copy(y[:, 2, :].rearrange("p (h s c) -> p h s c", h=2, c=2),
-                              sum2[:].rearrange("p (h c s) -> p h s c", h=2, c=2))
+        nc.scalar.copy(y[:, 0:2, :], sums01[:])
+        nc.vector.tensor_copy(y[:, 2, :], sum2[:])
         nc.sync.dma_start(out_by_r[:, 0:3, :], y[:, 0:3, :])
         last = [in_bank(BANK_LAST[h], [P, P], "last%d" % h) for h in range(2)]
         for h in range(2):
             mx_pass(last[h][:], columns(pv23, P, P), columns(wt, h * P, P), True, False)
         y_bf = alloc([P, 4 * Q], BF16, "y_bf")
-        y_dst = y_bf[:].rearrange("p (h s c r) -> p h s c r", h=2, c=2, r=4)
-        y_src = y[:].rearrange("p r (h s c) -> p h s c r", h=2, c=2)
-        nc.vector.tensor_copy(y_dst[:, 0, :, :, 0:3], y_src[:, 0, :, :, 0:3])
+        y_dst = y_bf[:].rearrange("p (h s r) -> p h s r", h=2, r=4)
+        y_src = y[:].rearrange("p r (h s) -> p h s r", h=2)
+        nc.vector.tensor_copy(y_dst[:, 0, :, 0:3], y_src[:, 0, :, 0:3])
 
         vt_bf3 = alloc([P, 1, 4 * P], BF16, "vt_bf3")
         weave(vt_bf3[:], turned3[:])
-        nc.scalar.copy(y_dst[:, 1, :, :, 0:3], y_src[:, 1, :, :, 0:3])
+        nc.scalar.copy(y_dst[:, 1, :, 0:3], y_src[:, 1, :, 0:3])
         vt3 = quantized(vt_bf3[:, 0, :], P, "vt3")
-        for h in range(2):
+        for h in (1, 0):
             mx_pass(last[h][:], columns(vt3, 0, P), columns(xt, h * P, P), False, True)
-        last_sums = [bank[:].rearrange("p (c s) -> p s c", c=2) for bank in last]
         copies = (nc.vector.tensor_copy, nc.scalar.copy)
         for h in range(2):
-            copies[h](y_dst[:, h, :, :, 3], last_sums[h])
-            copies[h](y_src[:, h, :, :, 3], last_sums[h])
+            copies[h](y_dst[:, h, :, 3], last[h][:])
+            copies[h](y_src[:, h, :, 3], last[h][:])
         nc.sync.dma_start(out_by_r[:, 3, :], y[:, 3, :])
         y_codes = alloc([P, Q], U32, "y_codes")
         y_scales = alloc([P, Q], U8, "y_scales")

@@ -20,18 +20,19 @@ ACT = mybir.ActivationFunctionType
 P = 128
 PREFIX, SUFFIX = 0, 1
 PK_SPLIT = 336
-PV_SPLIT = 40
+PV_SPLIT = 32
 LAST_GATHER_SPLIT = 16
 GUESS = 0.9375
 BANK_SCORE = [[0, 1], [2, 3]]
 BANK_WEIGHTS = [[4, 5], [0, 1]]
-BANK_VALS = [2, 6, 7]
-BANK_SUMS01, BANK_SUM2 = 6, 4
+BANK_VALS = [3, 6, 7]
+BANK_SUM0, BANK_SUMS12 = 6, 4
 BANK_LAST = [6, 4]
 BANK_LSE = 7
 AT_WINDOW = [None, None, 24576, 0]
 AT_APART, AT_PKEY = 8192, 49152
 AT_PVAL = 16384
+AT_LAST_WEAVE = 32768
 
 
 def tile_attend_cascade_pl_kernel(tc, query, pkey, pval, keys_words, keys_scales, vals, l1, l2, psz, size, offs,
@@ -160,12 +161,6 @@ def tile_attend_cascade_pl_kernel(tc, query, pkey, pval, keys_words, keys_scales
                 nc.scalar.activation(picked[:, cut:], windows[r][:].indirect(offsets[:, vector_columns:]), ACT.Copy)
             return [picked[:].bitcast(F32)[:, u:I // 2:2] for u in range(2)]
 
-        def gather_sorted(r):
-            picked = alloc([P, 2, P, 2], BF16, "picked%d" % r)
-            nc.vector.tensor_copy(picked[:].rearrange("p u s e -> p s u e"), windows[r][:].indirect(offsets[:]))
-            pairs = picked[:].rearrange("p u s e -> p u (s e)").bitcast(F32)
-            return [pairs[:, u, :] for u in range(2)]
-
         def turn(pairs, bank):
             for u in range(2):
                 nc.tensor.transpose(bank[:, u, :], pairs[u], ident[:])
@@ -187,13 +182,13 @@ def tile_attend_cascade_pl_kernel(tc, query, pkey, pval, keys_words, keys_scales
         kg_words = alloc([P, I], U16, "kg_words", AT_PKEY)
         nc.vector.tensor_copy(kg_words[:], key_words[:].indirect(offsets[:]))
         ex_prefix = [scores_exp(PREFIX, c, columns(pk, 0, M), FP8X4) for c in range(2)]
-        picked0 = gather_sorted(0)
+        picked0 = gather(0, I // 16)
         w_bf = alloc([P, 4 * Q], BF16, "w_bf")
         for c in range(2):
             weigh(PREFIX, c, turn_rows(PREFIX, c, ex_prefix[c]), w_bf)
         wt = quantized(w_bf[:], Q, "wt")
         ex_suffix = [scores_exp(SUFFIX, c, (kg_words[:], kg_scales[:]), FP4X4) for c in range(2)]
-        picked1 = gather_sorted(1)
+        picked1 = gather(1, I // 16)
         x_bf = alloc([P, 4 * Q], BF16, "x_bf")
         for c in range(2):
             weigh(SUFFIX, c, turn_rows(SUFFIX, c, ex_suffix[c]), x_bf)
@@ -206,6 +201,7 @@ def tile_attend_cascade_pl_kernel(tc, query, pkey, pval, keys_words, keys_scales
         turn(gather(2, 0), turned2[:, 0])
         vt_bf01 = alloc([P, 2, 4 * P], BF16, "vt_bf01", AT_WINDOW[2])
         weave(vt_bf01[:], turned01[:])
+        vt01 = quantized(vt_bf01[:].rearrange("p r w -> p (r w)"), 2 * P, "vt01")
         vt_bf2 = alloc([P, 1, 4 * P], BF16, "vt_bf2")
         weave(vt_bf2[:], turned2[:])
 
@@ -216,43 +212,40 @@ def tile_attend_cascade_pl_kernel(tc, query, pkey, pval, keys_words, keys_scales
         nc.vector.tensor_copy(pv_dst[0], pv_src[:, :, :, 0:2])
         nc.vector.tensor_copy(pv_dst[1][:, :PV_SPLIT], pv_src[:, :PV_SPLIT, :, 2:4])
         pv01 = quantized(pv_bf[0][:].rearrange("p r s j -> p (r s j)"), 2 * P, "pv01")
-        vt01 = quantized(vt_bf01[:].rearrange("p r w -> p (r w)"), 2 * P, "vt01", AT_PVAL)
         pv23 = quantized(pv_bf[1][:].rearrange("p r s j -> p (r s j)"), 2 * P, "pv23")
-        vt2 = quantized(vt_bf2[:, 0, :], P, "vt2", AT_PVAL + 1024)
+        vt2 = quantized(vt_bf2[:, 0, :], P, "vt2", AT_PVAL)
 
-        sums01 = in_bank(BANK_SUMS01, [P, 2, Q], "sums01")
-        for r in range(2):
-            mx_pass(sums01[:, r, :], columns(pv01, r * P, P), columns(wt, 0, Q), r == 0, False)
-        for r in range(2):
-            mx_pass(sums01[:, r, :], columns(vt01, r * P, P), columns(xt, 0, Q), False, r == 1)
-        sum2 = in_bank(BANK_SUM2, [P, Q], "sum2")
-        mx_pass(sum2[:], columns(pv23, 0, P), columns(wt, 0, Q), True, False)
-        mx_pass(sum2[:], columns(vt2, 0, P), columns(xt, 0, Q), False, True)
+        sum0 = in_bank(BANK_SUM0, [P, Q], "sum0")
+        sums12 = in_bank(BANK_SUMS12, [P, 2, Q], "sums12")
+        mx_pass(sum0[:], columns(vt01, 0, P), columns(xt, 0, Q), True, False)
+        mx_pass(sums12[:, 0, :], columns(vt01, P, P), columns(xt, 0, Q), True, False)
+        mx_pass(sum0[:], columns(pv01, 0, P), columns(wt, 0, Q), False, True)
+        mx_pass(sums12[:, 0, :], columns(pv01, P, P), columns(wt, 0, Q), False, False)
+        mx_pass(sums12[:, 1, :], columns(pv23, 0, P), columns(wt, 0, Q), False, False)
+        mx_pass(sums12[:, 1, :], columns(vt2, 0, P), columns(xt, 0, Q), False, True)
 
         turned3 = in_bank(BANK_VALS[2], [P, 1, 2, P], "turned_vals3")
         turn(gather(3, LAST_GATHER_SPLIT), turned3[:, 0])
         y = alloc([P, 4, Q], F32, "y", AT_WINDOW[3])
         out_by_r = out_0.rearrange("(p r) q -> p r q", r=4)
-        nc.scalar.copy(y[:, 0:2, :], sums01[:])
-        nc.vector.tensor_copy(y[:, 2, :], sum2[:])
+        nc.scalar.copy(y[:, 0, :], sum0[:])
+        nc.vector.tensor_copy(y[:, 1:3, :], sums12[:])
         nc.sync.dma_start(out_by_r[:, 0:3, :], y[:, 0:3, :])
         last = [in_bank(BANK_LAST[h], [P, P], "last%d" % h) for h in range(2)]
         for h in range(2):
             mx_pass(last[h][:], columns(pv23, P, P), columns(wt, h * P, P), True, False)
-        y_bf = alloc([P, 4 * Q], BF16, "y_bf")
-        y_dst = y_bf[:].rearrange("p (h s r) -> p h s r", h=2, r=4)
-        y_src = y[:].rearrange("p r (h s) -> p h s r", h=2)
-        nc.vector.tensor_copy(y_dst[:, 0, :, 0:3], y_src[:, 0, :, 0:3])
 
-        vt_bf3 = alloc([P, 1, 4 * P], BF16, "vt_bf3")
+        vt_bf3 = alloc([P, 1, 4 * P], BF16, "vt_bf3", AT_LAST_WEAVE)
         weave(vt_bf3[:], turned3[:])
-        nc.scalar.copy(y_dst[:, 1, :, 0:3], y_src[:, 1, :, 0:3])
         vt3 = quantized(vt_bf3[:, 0, :], P, "vt3")
         for h in (1, 0):
             mx_pass(last[h][:], columns(vt3, 0, P), columns(xt, h * P, P), False, True)
+        y_bf = [alloc([P, P, 4], BF16, "y_bf0", AT_LAST_WEAVE), alloc([P, P, 4], BF16, "y_bf1")]
+        y_src = y[:].rearrange("p r (h s) -> p h s r", h=2)
         copies = (nc.vector.tensor_copy, nc.scalar.copy)
         for h in range(2):
-            copies[h](y_dst[:, h, :, 3], last[h][:])
+            copies[h](y_bf[h][:, :, 0:3], y_src[:, h, :, 0:3])
+            copies[h](y_bf[h][:, :, 3], last[h][:])
             copies[h](y_src[:, h, :, 3], last[h][:])
         nc.sync.dma_start(out_by_r[:, 3, :], y[:, 3, :])
         y_codes = alloc([P, Q], U32, "y_codes")
@@ -260,7 +253,7 @@ def tile_attend_cascade_pl_kernel(tc, query, pkey, pval, keys_words, keys_scales
         for h in (1, 0):
             cols = slice(h * P, (h + 1) * P)
             nc.vector.quantize_mx(out=y_codes[:, cols].bitcast(FP8X4), scales=y_scales[:, cols],
-                                  in_=y_bf[:, 4 * h * P:4 * (h + 1) * P])
+                                  in_=y_bf[h][:].rearrange("p s r -> p (s r)"))
         nc.sync.dma_start(out_1[0].rearrange("p c r -> p (c r)").bitcast(I32), y_codes[:].bitcast(I32))
         for quad in range(4):
             queue = nc.scalar if quad % 2 == 0 else nc.sync

@@ -29,6 +29,7 @@ BANK_VALS = [3, 6, 7]
 BANK_SUM0, BANK_SUMS12 = 6, 4
 BANK_LAST = [6, 4]
 BANK_LSE = 7
+BANK_WARM = 5
 AT_WINDOW = [None, None, 24576, 0]
 AT_APART, AT_PKEY = 8192, 49152
 AT_PVAL = 16384
@@ -219,6 +220,9 @@ def tile_attend_cascade_pl_kernel(tc, query, pkey, pval, keys_words, keys_scales
         sums12 = in_bank(BANK_SUMS12, [P, 2, Q], "sums12")
         mx_pass(sum0[:], columns(vt01, 0, P), columns(xt, 0, Q), True, False)
         mx_pass(sums12[:, 0, :], columns(vt01, P, P), columns(xt, 0, Q), True, False)
+        warm = in_bank(BANK_WARM, [P, Q + P], "warm")
+        mx_pass(warm[:, :Q], columns(vt01, 0, P), columns(xt, 0, Q), True, True)
+        mx_pass(warm[:, Q:], columns(vt01, 0, P), columns(xt, 0, P), True, True)
         mx_pass(sum0[:], columns(pv01, 0, P), columns(wt, 0, Q), False, True)
         mx_pass(sums12[:, 0, :], columns(pv01, P, P), columns(wt, 0, Q), False, False)
         mx_pass(sums12[:, 1, :], columns(pv23, 0, P), columns(wt, 0, Q), False, False)

@@ -69,13 +69,13 @@ def tile_attend_cascade_pl_kernel(tc, query, pkey, pval, keys_words, keys_scales
         nc.sync.dma_start(q_raw[:], query.rearrange("(p j) q -> p j q", j=4))
         offsets = sb.tile([P, I // 16], U16, name="offsets")
         nc.sync.dma_start(offsets[:], offs)
-        key_scales = alloc([P, T], U8, "key_scales")
-        nc.vector.memset(key_scales[:].bitcast(I32), 0)
-        nc.sync.dma_start(key_scales[0:P:8, :].bitcast(I32), keys_scales[0].bitcast(I32))
         rows = alloc([P, P], F32, "rows")
         nc.gpsimd.memset(rows[:], 0.0)
         nc.sync.dma_start(rows[0:2, :], l1.rearrange("(c p) o -> c (p o)", c=2))
         nc.sync.dma_start(rows[2:4, :], l2.rearrange("(c p) o -> c (p o)", c=2))
+        key_scales = alloc([P, T], U8, "key_scales")
+        nc.gpsimd.memset(key_scales[:].bitcast(I32), 0)
+        nc.sync.dma_start(key_scales[0:P:8, :].bitcast(I32), keys_scales[0].bitcast(I32))
         token_w = [alloc([P, 4], F32, "psz_cols"), alloc([P, 4], F32, "size_cols")]
         vals_by_r = vals.rearrange("(p r) t -> r p t", r=4)
 

@@ -25,12 +25,13 @@ LAST_GATHER_SPLIT = 16
 GUESS = 0.9375
 BANK_SCORE = [[0, 1], [2, 3]]
 BANK_WEIGHTS = [[4, 5], [0, 1]]
-BANK_VALS = [3, 6, 7]
+BANK_VALS = [2, 3, 6, 7]
 BANK_SUM0, BANK_SUMS12 = 6, 4
 BANK_LAST = [6, 4]
 BANK_LSE = 7
 BANK_WARM = 5
 AT_WINDOW = [None, None, 24576, 0]
+AT_LAST_EXP = 40960
 AT_APART, AT_PKEY = 8192, 49152
 AT_PVAL = 16384
 AT_LAST_WEAVE = 32768
@@ -137,7 +138,7 @@ def tile_attend_cascade_pl_kernel(tc, query, pkey, pval, keys_words, keys_scales
         def scores_exp(part, c, keys, keys_dtype):
             bank = in_bank(BANK_SCORE[part][c], [P, 512], "score%d%d" % (part, c))
             mx_pass(bank[:], columns(qq, c * P, P), keys, True, True, keys_dtype)
-            ex = alloc([P, 512], F32, "ex%d%d" % (part, c))
+            ex = alloc([P, 512], F32, "ex%d%d" % (part, c), AT_LAST_EXP if (part, c) == (SUFFIX, 1) else None)
             nc.scalar.activation(ex[:].rearrange("q (t p) -> q t p", t=4),
                                  bank[:].rearrange("q (p t) -> q t p", t=4),
                                  ACT.Exp, bias=neg_lse[:, c:c + 1])
@@ -191,20 +192,24 @@ def tile_attend_cascade_pl_kernel(tc, query, pkey, pval, keys_words, keys_scales
         ex_suffix = [scores_exp(SUFFIX, c, (kg_words[:], kg_scales[:]), FP4X4) for c in range(2)]
         picked1 = gather(1, I // 16)
         x_bf = alloc([P, 4 * Q], BF16, "x_bf")
+        turned_suffix = [turn_rows(SUFFIX, 0, ex_suffix[0])]
+        turned = [in_bank(BANK_VALS[r], [P, 1, 2, P], "turned_vals%d" % r) for r in range(4)]
+        turn(picked0, turned[0][:, 0])
+        vt_bf0 = alloc([P, 1, 4 * P], BF16, "vt_bf0")
+        weave(vt_bf0[:], turned[0][:])
+        turned_suffix.append(turn_rows(SUFFIX, 1, ex_suffix[1]))
         for c in range(2):
-            weigh(SUFFIX, c, turn_rows(SUFFIX, c, ex_suffix[c]), x_bf)
+            weigh(SUFFIX, c, turned_suffix[c], x_bf)
+        vt0 = quantized(vt_bf0[:, 0, :], P, "vt0", AT_LAST_EXP)
         xt = quantized(x_bf[:], Q, "xt")
 
-        turned01 = in_bank(BANK_VALS[0], [P, 2, 2, P], "turned_vals01")
-        turn(picked0, turned01[:, 0])
-        turn(picked1, turned01[:, 1])
-        turned2 = in_bank(BANK_VALS[1], [P, 1, 2, P], "turned_vals2")
-        turn(gather(2, 0), turned2[:, 0])
-        vt_bf01 = alloc([P, 2, 4 * P], BF16, "vt_bf01", AT_WINDOW[2])
-        weave(vt_bf01[:], turned01[:])
-        vt01 = quantized(vt_bf01[:].rearrange("p r w -> p (r w)"), 2 * P, "vt01")
+        turn(picked1, turned[1][:, 0])
+        turn(gather(2, 0), turned[2][:, 0])
+        vt_bf1 = alloc([P, 1, 4 * P], BF16, "vt_bf1", AT_WINDOW[2])
+        weave(vt_bf1[:], turned[1][:])
+        vt1 = quantized(vt_bf1[:, 0, :], P, "vt1")
         vt_bf2 = alloc([P, 1, 4 * P], BF16, "vt_bf2")
-        weave(vt_bf2[:], turned2[:])
+        weave(vt_bf2[:], turned[2][:])
 
         pv_src = pv_raw[:].rearrange("p j (s r) -> p s j r", r=4)
         pv_bf = [alloc([P, 2, P, 4], BF16, "pv_bf%d" % h) for h in range(2)]
@@ -218,18 +223,17 @@ def tile_attend_cascade_pl_kernel(tc, query, pkey, pval, keys_words, keys_scales
 
         sum0 = in_bank(BANK_SUM0, [P, Q], "sum0")
         sums12 = in_bank(BANK_SUMS12, [P, 2, Q], "sums12")
-        mx_pass(sum0[:], columns(vt01, 0, P), columns(xt, 0, Q), True, False)
-        mx_pass(sums12[:, 0, :], columns(vt01, P, P), columns(xt, 0, Q), True, False)
+        mx_pass(sum0[:], columns(vt0, 0, P), columns(xt, 0, Q), True, False)
+        mx_pass(sums12[:, 0, :], columns(vt1, 0, P), columns(xt, 0, Q), True, False)
         warm = in_bank(BANK_WARM, [P, Q + P], "warm")
-        mx_pass(warm[:, :Q], columns(vt01, 0, P), columns(xt, 0, Q), True, True)
-        mx_pass(warm[:, Q:], columns(vt01, 0, P), columns(xt, 0, P), True, True)
+        mx_pass(warm[:, :Q], columns(vt1, 0, P), columns(xt, 0, Q), True, True)
+        mx_pass(warm[:, Q:], columns(vt1, 0, P), columns(xt, 0, P), True, True)
         mx_pass(sum0[:], columns(pv01, 0, P), columns(wt, 0, Q), False, True)
         mx_pass(sums12[:, 0, :], columns(pv01, P, P), columns(wt, 0, Q), False, False)
         mx_pass(sums12[:, 1, :], columns(pv23, 0, P), columns(wt, 0, Q), False, False)
         mx_pass(sums12[:, 1, :], columns(vt2, 0, P), columns(xt, 0, Q), False, True)
 
-        turned3 = in_bank(BANK_VALS[2], [P, 1, 2, P], "turned_vals3")
-        turn(gather(3, LAST_GATHER_SPLIT), turned3[:, 0])
+        turn(gather(3, LAST_GATHER_SPLIT), turned[3][:, 0])
         y = alloc([P, 4, Q], F32, "y", AT_WINDOW[3])
         out_by_r = out_0.rearrange("(p r) q -> p r q", r=4)
         nc.scalar.copy(y[:, 0, :], sum0[:])
@@ -240,7 +244,7 @@ def tile_attend_cascade_pl_kernel(tc, query, pkey, pval, keys_words, keys_scales
             mx_pass(last[h][:], columns(pv23, P, P), columns(wt, h * P, P), True, False)
 
         vt_bf3 = alloc([P, 1, 4 * P], BF16, "vt_bf3", AT_LAST_WEAVE)
-        weave(vt_bf3[:], turned3[:])
+        weave(vt_bf3[:], turned[3][:])
         vt3 = quantized(vt_bf3[:, 0, :], P, "vt3")
         for h in (1, 0):
             mx_pass(last[h][:], columns(vt3, 0, P), columns(xt, h * P, P), False, True)

@@ -28,9 +28,9 @@ BANK_WEIGHTS = [[4, 5], [0, 1]]
 BANK_VALS = [2, 3, 6, 7]
 BANK_SUM0, BANK_SUMS12 = 6, 4
 BANK_LAST = [6, 4]
-BANK_LSE = 7
+BANK_LSE, BANK_TOKENS = 7, 6
 BANK_WARM = 5
-AT_WINDOW = [None, None, 24576, 0]
+AT_WINDOW = [57344, 65536, 24576, 0]
 AT_LAST_EXP = 40960
 AT_APART, AT_PKEY = 8192, 49152
 AT_PVAL = 16384
@@ -66,10 +66,10 @@ def tile_attend_cascade_pl_kernel(tc, query, pkey, pval, keys_words, keys_scales
             nc.tensor.matmul_mx(out=out, lhsT=stationary[0].bitcast(FP8X4), lhsT_scale=stationary[1],
                                 rhs=moving[0].bitcast(moving_dtype), rhs_scale=moving[1], start=start, stop=stop)
 
-        q_raw = alloc([P, 4, Q], F32, "q_raw")
-        nc.sync.dma_start(q_raw[:], query.rearrange("(p j) q -> p j q", j=4))
         offsets = sb.tile([P, I // 16], U16, name="offsets")
         nc.sync.dma_start(offsets[:], offs)
+        q_raw = alloc([P, 4, Q], F32, "q_raw")
+        nc.sync.dma_start(q_raw[:], query.rearrange("(p j) q -> p j q", j=4))
         rows = alloc([P, P], F32, "rows")
         nc.gpsimd.memset(rows[:], 0.0)
         nc.sync.dma_start(rows[0:2, :], l1.rearrange("(c p) o -> c (p o)", c=2))
@@ -77,7 +77,6 @@ def tile_attend_cascade_pl_kernel(tc, query, pkey, pval, keys_words, keys_scales
         key_scales = alloc([P, T], U8, "key_scales")
         nc.gpsimd.memset(key_scales[:].bitcast(I32), 0)
         nc.sync.dma_start(key_scales[0:P:8, :].bitcast(I32), keys_scales[0].bitcast(I32))
-        token_w = [alloc([P, 4], F32, "psz_cols"), alloc([P, 4], F32, "size_cols")]
         vals_by_r = vals.rearrange("(p r) t -> r p t", r=4)
 
         def load_window(r):
@@ -87,10 +86,15 @@ def tile_attend_cascade_pl_kernel(tc, query, pkey, pval, keys_words, keys_scales
 
         pk_raw = alloc([P, 4, M], F32, "pk_raw", AT_PKEY)
         nc.sync.dma_start(pk_raw[:], pkey.rearrange("(p j) m -> p j m", j=4))
+        ident = alloc([P, P], F32, "ident")
+        make_identity(nc, ident[:])
+        token_rows = alloc([P, 512], F32, "token_rows")
+        nc.gpsimd.memset(token_rows[:], 0.0)
+        nc.sync.dma_start(token_rows[PREFIX:PREFIX + 1, :], psz)
+        nc.sync.dma_start(token_rows[SUFFIX:SUFFIX + 1, :], size)
         key_words = alloc([P, T], U16, "key_words")
         nc.sync.dma_start(key_words[:].bitcast(I32), keys_words[0].bitcast(I32))
         windows = [load_window(0)]
-        nc.sync.dma_start(token_w[PREFIX][:], psz.rearrange("o (p t) -> p (o t)", t=4))
         kg_rows = alloc([P, I], U8, "kg_rows")
         nc.vector.tensor_copy(kg_rows[:], key_scales[:].indirect(offsets[:]))
         kg_scales = alloc([P, I], U8, "kg_scales")
@@ -98,17 +102,17 @@ def tile_attend_cascade_pl_kernel(tc, query, pkey, pval, keys_words, keys_scales
         for j in range(1, 4):
             nc.sync.dma_start(kg_scales[j:P:32, :].bitcast(I32), kg_rows[8 * j:P:32, :].bitcast(I32))
         windows.append(load_window(1))
-        nc.sync.dma_start(token_w[SUFFIX][:], size.rearrange("o (p t) -> p (o t)", t=4))
         windows.append(load_window(2))
         pv_raw = alloc([P, 4, E], F32, "pv_raw", AT_PVAL)
         nc.sync.dma_start(pv_raw[:], pval.rearrange("(p j) e -> p j e", j=4))
         windows.append(load_window(3))
-        ident = alloc([P, P], F32, "ident")
-        make_identity(nc, ident[:])
 
         lse_bank = in_bank(BANK_LSE, [P, P], "lse_columns")
         nc.tensor.transpose(lse_bank[:], rows[:], ident[:])
         lse = [lse_bank[:, 0:2], lse_bank[:, 2:4]]
+        token_bank = in_bank(BANK_TOKENS, [P, 4, P], "token_columns")
+        for t in range(4):
+            nc.tensor.transpose(token_bank[:, t, :], token_rows[:, t:512:4], ident[:])
 
         def small(name, at=None):
             return alloc([P, 2], F32, name, at)
@@ -152,7 +156,7 @@ def tile_attend_cascade_pl_kernel(tc, query, pkey, pval, keys_words, keys_scales
 
         def weigh(part, c, bank, w_bf):
             nc.vector.tensor_tensor(w_bf[:].rearrange("p (c s t) -> p c s t", c=2, t=4)[:, c], bank[:].rearrange("p t s -> p s t"),
-                                    token_w[part][:].unsqueeze(1).to_broadcast([P, P, 4]), ALU.mult)
+                                    token_w[:, part, :].unsqueeze(1).to_broadcast([P, P, 4]), ALU.mult)
 
         def gather(r, vector_columns):
             picked = alloc([P, I], BF16, "picked%d" % r)
@@ -181,17 +185,19 @@ def tile_attend_cascade_pl_kernel(tc, query, pkey, pval, keys_words, keys_scales
         for c in range(2):
             nc.scalar.activation(neg_lse[:, c:c + 1], back1[:, c:c + 1], ACT.Identity,
                                  scale=slope[:, c:c + 1], bias=keep1[:, c:c + 1])
+        token_w = alloc([P, 2, 4], F32, "token_w", AT_PKEY + 1024)
+        nc.scalar.copy(token_w[:], token_bank[:, :, 0:2].rearrange("p t k -> p k t"))
         kg_words = alloc([P, I], U16, "kg_words", AT_PKEY)
         nc.vector.tensor_copy(kg_words[:], key_words[:].indirect(offsets[:]))
         ex_prefix = [scores_exp(PREFIX, c, columns(pk, 0, M), FP8X4) for c in range(2)]
         picked0 = gather(0, I // 16)
-        w_bf = alloc([P, 4 * Q], BF16, "w_bf")
+        w_bf = alloc([P, 4 * Q], BF16, "w_bf", AT_WINDOW[0])
         for c in range(2):
             weigh(PREFIX, c, turn_rows(PREFIX, c, ex_prefix[c]), w_bf)
-        wt = quantized(w_bf[:], Q, "wt")
         ex_suffix = [scores_exp(SUFFIX, c, (kg_words[:], kg_scales[:]), FP4X4) for c in range(2)]
         picked1 = gather(1, I // 16)
-        x_bf = alloc([P, 4 * Q], BF16, "x_bf")
+        wt = quantized(w_bf[:], Q, "wt", AT_WINDOW[1] + 2048)
+        x_bf = alloc([P, 4 * Q], BF16, "x_bf", AT_WINDOW[1])
         turned_suffix = [turn_rows(SUFFIX, 0, ex_suffix[0])]
         turned = [in_bank(BANK_VALS[r], [P, 1, 2, P], "turned_vals%d" % r) for r in range(4)]
         turn(picked0, turned[0][:, 0])

@@ -66,10 +66,10 @@ def tile_attend_cascade_pl_kernel(tc, query, pkey, pval, keys_words, keys_scales
             nc.tensor.matmul_mx(out=out, lhsT=stationary[0].bitcast(FP8X4), lhsT_scale=stationary[1],
                                 rhs=moving[0].bitcast(moving_dtype), rhs_scale=moving[1], start=start, stop=stop)
 
-        offsets = sb.tile([P, I // 16], U16, name="offsets")
-        nc.sync.dma_start(offsets[:], offs)
         q_raw = alloc([P, 4, Q], F32, "q_raw")
         nc.sync.dma_start(q_raw[:], query.rearrange("(p j) q -> p j q", j=4))
+        offsets = sb.tile([P, I // 16], U16, name="offsets")
+        nc.sync.dma_start(offsets[:], offs)
         rows = alloc([P, P], F32, "rows")
         nc.gpsimd.memset(rows[:], 0.0)
         nc.sync.dma_start(rows[0:2, :], l1.rearrange("(c p) o -> c (p o)", c=2))
@@ -86,10 +86,10 @@ def tile_attend_cascade_pl_kernel(tc, query, pkey, pval, keys_words, keys_scales
 
         pk_raw = alloc([P, 4, M], F32, "pk_raw", AT_PKEY)
         nc.sync.dma_start(pk_raw[:], pkey.rearrange("(p j) m -> p j m", j=4))
-        ident = alloc([P, P], F32, "ident")
-        make_identity(nc, ident[:])
         token_rows = alloc([P, 512], F32, "token_rows")
         nc.gpsimd.memset(token_rows[:], 0.0)
+        ident = alloc([P, P], F32, "ident")
+        make_identity(nc, ident[:])
         nc.sync.dma_start(token_rows[PREFIX:PREFIX + 1, :], psz)
         nc.sync.dma_start(token_rows[SUFFIX:SUFFIX + 1, :], size)
         key_words = alloc([P, T], U16, "key_words")

@@ -122,11 +122,11 @@ def tile_attend_cascade_pl_kernel(tc, query, pkey, pval, keys_words, keys_scales
         for c in range(2):
             nc.scalar.activation(apart[:, c:c + 1], lse[SUFFIX][:, c:c + 1], ACT.Abs, bias=neg_l1[:, c:c + 1])
         nc.scalar.activation(ratio[:], apart[:], ACT.Exp, scale=-1.0)
-        nc.scalar.activation(slope[:], ratio[:], ACT.Identity, scale=-1.0, bias=-1.0)
         neg_top, square, back0, step1, keep1 = small("neg_top"), small("square"), small("back0"), small("step1"), small("keep1")
         rest = small("rest")
         nc.vector.scalar_tensor_tensor(neg_top[:], lse[SUFFIX], -1.0, neg_l1[:], ALU.mult, ALU.min)
         nc.vector.tensor_scalar_add(rest[:], neg_top[:], 2.0 - GUESS * GUESS)
+        nc.vector.tensor_scalar(slope[:], ratio[:], -1.0, -1.0, ALU.mult, ALU.add)
         nc.scalar.activation(square[:], ratio[:], ACT.Square, scale=0.5, bias=-GUESS)
         nc.scalar.activation(back0[:], square[:], ACT.Exp, bias=-GUESS * GUESS)
         for c in range(2):
@@ -186,7 +186,7 @@ def tile_attend_cascade_pl_kernel(tc, query, pkey, pval, keys_words, keys_scales
             nc.scalar.activation(neg_lse[:, c:c + 1], back1[:, c:c + 1], ACT.Identity,
                                  scale=slope[:, c:c + 1], bias=keep1[:, c:c + 1])
         token_w = alloc([P, 2, 4], F32, "token_w", AT_PKEY + 1024)
-        nc.scalar.copy(token_w[:], token_bank[:, :, 0:2].rearrange("p t k -> p k t"))
+        nc.vector.tensor_copy(token_w[:], token_bank[:, :, 0:2].rearrange("p t k -> p k t"))
         kg_words = alloc([P, I], U16, "kg_words", AT_PKEY)
         nc.vector.tensor_copy(kg_words[:], key_words[:].indirect(offsets[:]))
         ex_prefix = [scores_exp(PREFIX, c, columns(pk, 0, M), FP8X4) for c in range(2)]
@@ -250,9 +250,13 @@ def tile_attend_cascade_pl_kernel(tc, query, pkey, pval, keys_words, keys_scales
             mx_pass(last[h][:], columns(pv23, P, P), columns(wt, h * P, P), True, False)
 
         vt_bf3 = alloc([P, 1, 4 * P], BF16, "vt_bf3", AT_LAST_WEAVE)
-        weave(vt_bf3[:], turned[3][:])
-        vt3 = quantized(vt_bf3[:, 0, :], P, "vt3")
-        for h in (1, 0):
+        vt3 = (alloc([P, P], U32, "vt3_codes"), alloc([P, P], U8, "vt3_scales"))
+        for first in (0, P // 2):
+            weave(vt_bf3[:, :, 4 * first:4 * first + 2 * P], turned[3][:, :, :, first:first + P // 2])
+        for first in (0, P // 2):
+            codes, scales = columns(vt3, first, P // 2)
+            nc.vector.quantize_mx(out=codes.bitcast(FP8X4), scales=scales, in_=vt_bf3[:, 0, 4 * first:4 * first + 2 * P])
+        for h in range(2):
             mx_pass(last[h][:], columns(vt3, 0, P), columns(xt, h * P, P), False, True)
         y_bf = [alloc([P, P, 4], BF16, "y_bf0", AT_LAST_WEAVE), alloc([P, P, 4], BF16, "y_bf1")]
         y_src = y[:].rearrange("p r (h s) -> p h s r", h=2)
@@ -270,5 +274,5 @@ def tile_attend_cascade_pl_kernel(tc, query, pkey, pval, keys_words, keys_scales
                                   in_=y_bf[h][:].rearrange("p s r -> p (s r)"))
         nc.sync.dma_start(out_1[0].rearrange("p c r -> p (c r)").bitcast(I32), y_codes[:].bitcast(I32))
         for quad in range(4):
-            queue = nc.scalar if quad % 2 == 0 else nc.sync
+            queue = nc.scalar if quad < 3 else nc.sync
             queue.dma_start(out_2[0, quad:16:4, :].bitcast(I32), y_scales[quad:P:32, :].bitcast(I32))

from contextlib import ExitStack

import concourse.mybir as mybir
from concourse.masks import make_identity

D, T, I, Q, E, M = 512, 2048, 512, 256, 512, 512
FLOPS = 2 * (D * Q * M + D * Q * I + M * E * Q + I * E * Q)

F32 = mybir.dt.float32
BF16 = mybir.dt.bfloat16
I32 = mybir.dt.int32
U32 = mybir.dt.uint32
U16 = mybir.dt.uint16
U8 = mybir.dt.uint8
FP8X4 = mybir.dt.float8_e4m3fn_x4
FP4X4 = mybir.dt.float4_e2m1fn_x4
ALU = mybir.AluOpType
ACT = mybir.ActivationFunctionType

P = 128
PREFIX, SUFFIX = 0, 1
PK_SPLIT = 336
PV_SPLIT = 32
LAST_GATHER_SPLIT = 16
GUESS = 0.9375
BANK_SCORE = [[0, 1], [2, 3]]
BANK_WEIGHTS = [[4, 5], [0, 1]]
BANK_VALS = [2, 3, 6, 7]
BANK_SUM0, BANK_SUMS12 = 6, 4
BANK_LAST = [6, 4]
BANK_LSE, BANK_TOKENS = 7, 6
BANK_WARM = 5
AT_WINDOW = [57344, 65536, 24576, 0]
AT_LAST_EXP = 40960
AT_APART, AT_PKEY = 8192, 49152
AT_PVAL = 16384
AT_LAST_WEAVE = 32768


def tile_attend_cascade_pl_kernel(tc, query, pkey, pval, keys_words, keys_scales, vals, l1, l2, psz, size, offs,
                                       out_0, out_1, out_2):
    nc = tc.nc
    with ExitStack() as ctx:
        sb = ctx.enter_context(tc.tile_pool(name="sb", bufs=1))
        reused = ctx.enter_context(tc.tile_pool(name="reused", bufs=1))
        psum = ctx.enter_context(tc.psum_pool(name="psum", bufs=1))

        def in_bank(bank, shape, name):
            return psum.tile(shape, F32, name=name, offset=2048 * bank)

        def alloc(shape, dtype, name, at=None):
            if at is None:
                return sb.tile(shape, dtype, name=name, align_bytes=64)
            return reused.tile(shape, dtype, name=name, align_bytes=64, offset=at)

        def quantized(values, width, name, at=None):
            codes = alloc([P, width], U32, name + "_codes", at)
            scales = alloc([P, width], U8, name + "_scales")
            nc.vector.quantize_mx(out=codes[:].bitcast(FP8X4), scales=scales[:], in_=values)
            return codes, scales

        def columns(operand, first, count):
            return operand[0][:, first:first + count], operand[1][:, first:first + count]

        def mx_pass(out, stationary, moving, start, stop, moving_dtype=FP8X4):
            nc.tensor.matmul_mx(out=out, lhsT=stationary[0].bitcast(FP8X4), lhsT_scale=stationary[1],
                                rhs=moving[0].bitcast(moving_dtype), rhs_scale=moving[1], start=start, stop=stop)

        q_raw = alloc([P, 4, Q], F32, "q_raw")
        nc.sync.dma_start(q_raw[:], query.rearrange("(p j) q -> p j q", j=4))
        offsets = sb.tile([P, I // 16], U16, name="offsets")
        nc.sync.dma_start(offsets[:], offs)
        rows = alloc([P, P], F32, "rows")
        nc.gpsimd.memset(rows[:], 0.0)
        nc.sync.dma_start(rows[0:2, :], l1.rearrange("(c p) o -> c (p o)", c=2))
        nc.sync.dma_start(rows[2:4, :], l2.rearrange("(c p) o -> c (p o)", c=2))
        key_scales = alloc([P, T], U8, "key_scales")
        nc.gpsimd.memset(key_scales[:].bitcast(I32), 0)
        nc.sync.dma_start(key_scales[0:P:8, :].bitcast(I32), keys_scales[0].bitcast(I32))
        vals_by_r = vals.rearrange("(p r) t -> r p t", r=4)

        def load_window(r):
            window = alloc([P, T], F32, "window%d" % r, AT_WINDOW[r])
            nc.sync.dma_start(window[:], vals_by_r[r])
            return window

        pk_raw = alloc([P, 4, M], F32, "pk_raw", AT_PKEY)
        nc.sync.dma_start(pk_raw[:], pkey.rearrange("(p j) m -> p j m", j=4))
        token_rows = alloc([P, 512], F32, "token_rows")
        nc.gpsimd.memset(token_rows[:], 0.0)
        ident = alloc([P, P], F32, "ident")
        make_identity(nc, ident[:])
        nc.sync.dma_start(token_rows[PREFIX:PREFIX + 1, :], psz)
        nc.sync.dma_start(token_rows[SUFFIX:SUFFIX + 1, :], size)
        key_words = alloc([P, T], U16, "key_words")
        nc.sync.dma_start(key_words[:].bitcast(I32), keys_words[0].bitcast(I32))
        windows = [load_window(0)]
        kg_rows = alloc([P, I], U8, "kg_rows")
        nc.vector.tensor_copy(kg_rows[:], key_scales[:].indirect(offsets[:]))
        kg_scales = alloc([P, I], U8, "kg_scales")
        nc.vector.tensor_copy(kg_scales[:].bitcast(I32), kg_rows[:].bitcast(I32))
        for j in range(1, 4):
            nc.sync.dma_start(kg_scales[j:P:32, :].bitcast(I32), kg_rows[8 * j:P:32, :].bitcast(I32))
        windows.append(load_window(1))
        windows.append(load_window(2))
        pv_raw = alloc([P, 4, E], F32, "pv_raw", AT_PVAL)
        nc.sync.dma_start(pv_raw[:], pval.rearrange("(p j) e -> p j e", j=4))
        windows.append(load_window(3))

        lse_bank = in_bank(BANK_LSE, [P, P], "lse_columns")
        nc.tensor.transpose(lse_bank[:], rows[:], ident[:])
        lse = [lse_bank[:, 0:2], lse_bank[:, 2:4]]
        token_bank = in_bank(BANK_TOKENS, [P, 4, P], "token_columns")
        for t in range(4):
            nc.tensor.transpose(token_bank[:, t, :], token_rows[:, t:512:4], ident[:])

        def small(name, at=None):
            return alloc([P, 2], F32, name, at)

        neg_l1, apart, ratio, slope = small("neg_l1"), small("apart", AT_APART), small("ratio"), small("slope")
        nc.scalar.activation(neg_l1[:], lse[PREFIX], ACT.Identity, scale=-1.0)
        for c in range(2):
            nc.scalar.activation(apart[:, c:c + 1], lse[SUFFIX][:, c:c + 1], ACT.Abs, bias=neg_l1[:, c:c + 1])
        nc.scalar.activation(ratio[:], apart[:], ACT.Exp, scale=-1.0)
        neg_top, square, back0, step1, keep1 = small("neg_top"), small("square"), small("back0"), small("step1"), small("keep1")
        rest = small("rest")
        nc.vector.scalar_tensor_tensor(neg_top[:], lse[SUFFIX], -1.0, neg_l1[:], ALU.mult, ALU.min)
        nc.vector.tensor_scalar_add(rest[:], neg_top[:], 2.0 - GUESS * GUESS)
        nc.vector.tensor_scalar(slope[:], ratio[:], -1.0, -1.0, ALU.mult, ALU.add)
        nc.scalar.activation(square[:], ratio[:], ACT.Square, scale=0.5, bias=-GUESS)
        nc.scalar.activation(back0[:], square[:], ACT.Exp, bias=-GUESS * GUESS)
        for c in range(2):
            nc.scalar.activation(step1[:, c:c + 1], back0[:, c:c + 1], ACT.Identity,
                                 scale=slope[:, c:c + 1], bias=square[:, c:c + 1])
        for c in range(2):
            nc.scalar.activation(keep1[:, c:c + 1], step1[:, c:c + 1], ACT.Identity, bias=rest[:, c:c + 1])

        q_bf = alloc([P, 4 * Q], BF16, "q_bf")
        nc.scalar.copy(q_bf[:].rearrange("p (a i j) -> p a j i", i=4, j=4), q_raw[:].rearrange("p j (a i) -> p a j i", i=4))
        qq = quantized(q_bf[:], Q, "q")

        def scores_exp(part, c, keys, keys_dtype):
            bank = in_bank(BANK_SCORE[part][c], [P, 512], "score%d%d" % (part, c))
            mx_pass(bank[:], columns(qq, c * P, P), keys, True, True, keys_dtype)
            ex = alloc([P, 512], F32, "ex%d%d" % (part, c), AT_LAST_EXP if (part, c) == (SUFFIX, 1) else None)
            nc.scalar.activation(ex[:].rearrange("q (t p) -> q t p", t=4),
                                 bank[:].rearrange("q (p t) -> q t p", t=4),
                                 ACT.Exp, bias=neg_lse[:, c:c + 1])
            return ex

        def turn_rows(part, c, ex):
            bank = in_bank(BANK_WEIGHTS[part][c], [P, 4, P], "turned%d%d" % (part, c))
            for t in range(4):
                nc.tensor.transpose(bank[:, t, :], ex[:, t * P:(t + 1) * P], ident[:])
            return bank

        def weigh(part, c, bank, w_bf):
            nc.vector.tensor_tensor(w_bf[:].rearrange("p (c s t) -> p c s t", c=2, t=4)[:, c], bank[:].rearrange("p t s -> p s t"),
                                    token_w[:, part, :].unsqueeze(1).to_broadcast([P, P, 4]), ALU.mult)

        def gather(r, vector_columns):
            picked = alloc([P, I], BF16, "picked%d" % r)
            cut = 16 * vector_columns
            if cut > 0:
                nc.vector.tensor_copy(picked[:, :cut], windows[r][:].indirect(offsets[:, :vector_columns]))
            if cut < I:
                nc.scalar.activation(picked[:, cut:], windows[r][:].indirect(offsets[:, vector_columns:]), ACT.Copy)
            return [picked[:].bitcast(F32)[:, u:I // 2:2] for u in range(2)]

        def turn(pairs, bank):
            for u in range(2):
                nc.tensor.transpose(bank[:, u, :], pairs[u], ident[:])

        def weave(vt_bf, bank):
            nc.scalar.copy(vt_bf.bitcast(F32).rearrange("p r (s u) -> p r s u", u=2), bank.rearrange("p r u s -> p r s u"))

        pk_bf = alloc([P, 4 * M], BF16, "pk_bf", AT_APART)
        pk_dst = pk_bf[:].rearrange("p (a i j) -> p a j i", i=4, j=4)
        pk_src = pk_raw[:].rearrange("p j (a i) -> p a j i", i=4)
        nc.vector.tensor_copy(pk_dst[:, :PK_SPLIT // 4, :, :], pk_src[:, :PK_SPLIT // 4, :, :])
        nc.scalar.copy(pk_dst[:, PK_SPLIT // 4:, :, :], pk_src[:, PK_SPLIT // 4:, :, :])
        pk = quantized(pk_bf[:], M, "pk")
        back1, neg_lse = small("back1"), small("neg_lse")
        nc.scalar.activation(back1[:], step1[:], ACT.Exp, bias=1.0 - GUESS * GUESS)
        for c in range(2):
            nc.scalar.activation(neg_lse[:, c:c + 1], back1[:, c:c + 1], ACT.Identity,
                                 scale=slope[:, c:c + 1], bias=keep1[:, c:c + 1])
        token_w = alloc([P, 2, 4], F32, "token_w", AT_PKEY + 1024)
        nc.vector.tensor_copy(token_w[:], token_bank[:, :, 0:2].rearrange("p t k -> p k t"))
        kg_words = alloc([P, I], U16, "kg_words", AT_PKEY)
        nc.vector.tensor_copy(kg_words[:], key_words[:].indirect(offsets[:]))
        ex_prefix = [scores_exp(PREFIX, c, columns(pk, 0, M), FP8X4) for c in range(2)]
        picked0 = gather(0, I // 16)
        w_bf = alloc([P, 4 * Q], BF16, "w_bf", AT_WINDOW[0])
        for c in range(2):
            weigh(PREFIX, c, turn_rows(PREFIX, c, ex_prefix[c]), w_bf)
        ex_suffix = [scores_exp(SUFFIX, c, (kg_words[:], kg_scales[:]), FP4X4) for c in range(2)]
        picked1 = gather(1, I // 16)
        wt = quantized(w_bf[:], Q, "wt", AT_WINDOW[1] + 2048)
        x_bf = alloc([P, 4 * Q], BF16, "x_bf", AT_WINDOW[1])
        turned_suffix = [turn_rows(SUFFIX, 0, ex_suffix[0])]
        turned = [in_bank(BANK_VALS[r], [P, 1, 2, P], "turned_vals%d" % r) for r in range(4)]
        turn(picked0, turned[0][:, 0])
        vt_bf0 = alloc([P, 1, 4 * P], BF16, "vt_bf0")
        weave(vt_bf0[:], turned[0][:])
        turned_suffix.append(turn_rows(SUFFIX, 1, ex_suffix[1]))
        for c in range(2):
            weigh(SUFFIX, c, turned_suffix[c], x_bf)
        vt0 = quantized(vt_bf0[:, 0, :], P, "vt0", AT_LAST_EXP)
        xt = quantized(x_bf[:], Q, "xt")

        turn(picked1, turned[1][:, 0])
        turn(gather(2, 0), turned[2][:, 0])
        vt_bf1 = alloc([P, 1, 4 * P], BF16, "vt_bf1", AT_WINDOW[2])
        weave(vt_bf1[:], turned[1][:])
        vt1 = quantized(vt_bf1[:, 0, :], P, "vt1")
        vt_bf2 = alloc([P, 1, 4 * P], BF16, "vt_bf2")
        weave(vt_bf2[:], turned[2][:])

        pv_src = pv_raw[:].rearrange("p j (s r) -> p s j r", r=4)
        pv_bf = [alloc([P, 2, P, 4], BF16, "pv_bf%d" % h) for h in range(2)]
        pv_dst = [t[:].rearrange("p r s j -> p s j r") for t in pv_bf]
        nc.scalar.copy(pv_dst[1][:, PV_SPLIT:], pv_src[:, PV_SPLIT:, :, 2:4])
        nc.vector.tensor_copy(pv_dst[0], pv_src[:, :, :, 0:2])
        nc.vector.tensor_copy(pv_dst[1][:, :PV_SPLIT], pv_src[:, :PV_SPLIT, :, 2:4])
        pv01 = quantized(pv_bf[0][:].rearrange("p r s j -> p (r s j)"), 2 * P, "pv01")
        pv23 = quantized(pv_bf[1][:].rearrange("p r s j -> p (r s j)"), 2 * P, "pv23")
        vt2 = quantized(vt_bf2[:, 0, :], P, "vt2", AT_PVAL)

        sum0 = in_bank(BANK_SUM0, [P, Q], "sum0")
        sums12 = in_bank(BANK_SUMS12, [P, 2, Q], "sums12")
        mx_pass(sum0[:], columns(vt0, 0, P), columns(xt, 0, Q), True, False)
        mx_pass(sums12[:, 0, :], columns(vt1, 0, P), columns(xt, 0, Q), True, False)
        warm = in_bank(BANK_WARM, [P, Q + P], "warm")
        mx_pass(warm[:, :Q], columns(vt1, 0, P), columns(xt, 0, Q), True, True)
        mx_pass(warm[:, Q:], columns(vt1, 0, P), columns(xt, 0, P), True, True)
        mx_pass(sum0[:], columns(pv01, 0, P), columns(wt, 0, Q), False, True)
        mx_pass(sums12[:, 0, :], columns(pv01, P, P), columns(wt, 0, Q), False, False)
        mx_pass(sums12[:, 1, :], columns(pv23, 0, P), columns(wt, 0, Q), False, False)
        mx_pass(sums12[:, 1, :], columns(vt2, 0, P), columns(xt, 0, Q), False, True)

        turn(gather(3, LAST_GATHER_SPLIT), turned[3][:, 0])
        y = alloc([P, 4, Q], F32, "y", AT_WINDOW[3])
        out_by_r = out_0.rearrange("(p r) q -> p r q", r=4)
        nc.scalar.copy(y[:, 0, :], sum0[:])
        nc.vector.tensor_copy(y[:, 1:3, :], sums12[:])
        nc.sync.dma_start(out_by_r[:, 0:3, :], y[:, 0:3, :])
        last = [in_bank(BANK_LAST[h], [P, P], "last%d" % h) for h in range(2)]
        for h in range(2):
            mx_pass(last[h][:], columns(pv23, P, P), columns(wt, h * P, P), True, False)

        vt_bf3 = alloc([P, 1, 4 * P], BF16, "vt_bf3", AT_LAST_WEAVE)
        vt3 = (alloc([P, P], U32, "vt3_codes"), alloc([P, P], U8, "vt3_scales"))
        for first in (0, P // 2):
            weave(vt_bf3[:, :, 4 * first:4 * first + 2 * P], turned[3][:, :, :, first:first + P // 2])
        for first in (0, P // 2):
            codes, scales = columns(vt3, first, P // 2)
            nc.vector.quantize_mx(out=codes.bitcast(FP8X4), scales=scales, in_=vt_bf3[:, 0, 4 * first:4 * first + 2 * P])
        for h in range(2):
            mx_pass(last[h][:], columns(vt3, 0, P), columns(xt, h * P, P), False, True)
        y_bf = [alloc([P, P, 4], BF16, "y_bf0", AT_LAST_WEAVE), alloc([P, P, 4], BF16, "y_bf1")]
        y_src = y[:].rearrange("p r (h s) -> p h s r", h=2)
        copies = (nc.vector.tensor_copy, nc.scalar.copy)
        for h in range(2):
            copies[h](y_bf[h][:, :, 0:3], y_src[:, h, :, 0:3])
            copies[h](y_bf[h][:, :, 3], last[h][:])
            copies[h](y_src[:, h, :, 3], last[h][:])
        nc.sync.dma_start(out_by_r[:, 3, :], y[:, 3, :])
        y_codes = alloc([P, Q], U32, "y_codes")
        y_scales = alloc([P, Q], U8, "y_scales")
        for h in (1, 0):
            cols = slice(h * P, (h + 1) * P)
            nc.vector.quantize_mx(out=y_codes[:, cols].bitcast(FP8X4), scales=y_scales[:, cols],
                                  in_=y_bf[h][:].rearrange("p s r -> p (s r)"))
        nc.sync.dma_start(out_1[0].rearrange("p c r -> p (c r)").bitcast(I32), y_codes[:].bitcast(I32))
        for quad in range(4):
            queue = nc.scalar if quad < 3 else nc.sync
            queue.dma_start(out_2[0, quad:16:4, :].bitcast(I32), y_scales[quad:P:32, :].bitcast(I32))
